import numpy as np
import ml_dtypes


def mxq(x, axis, fmt="e4m3"):
    dtype, down = {"e4m3": (ml_dtypes.float8_e4m3fn, 7), "e5m2": (ml_dtypes.float8_e5m2, 14)}[fmt]
    v = np.moveaxis(np.asarray(x, np.float32).astype(ml_dtypes.bfloat16).astype(np.float64), axis, -1)
    blocks = v.reshape(v.shape[:-1] + (-1, 32))
    amax = np.abs(blocks).max(-1, keepdims=True)
    byte = np.maximum(np.where(amax > 0, np.frexp(amax)[1] - 1 + 127, 0) - down, 1)
    scale = np.exp2(byte - 127.0)
    codes = (blocks / scale).astype(np.float32).astype(dtype).astype(np.float64)
    return np.moveaxis((codes * scale).reshape(v.shape), -1, axis)


WIDE = False


def mx_kscale(k):
    if not WIDE:
        return np.ones(k)
    levels = np.array([10, -10, 5, -5, 0])
    if k % 512:
        return np.exp2(np.random.permutation(np.resize(levels, k // 32))).repeat(32)
    a = np.empty((k // 512, 16))
    for p in range(k // 512):
        a[p, :8] = np.random.permutation(np.resize(levels, 8))
        for g in range(8):
            far = levels[np.abs(levels - a[p, g]) >= 10]
            a[p, g + 8] = far[np.random.randint(len(far))]
    return np.exp2(a.ravel()).repeat(32)


BF16 = ml_dtypes.bfloat16


def bf(x):
    return np.asarray(x, np.float32).astype(BF16)


def f64(x):
    return np.asarray(x).astype(np.float64)


E2M1 = np.array([0.0, 0.5, 1.0, 1.5, 2.0, 3.0, 4.0, 6.0, -0.0, -0.5, -1.0, -1.5, -2.0, -3.0, -4.0, -6.0])


def pack_weight(w, fmt):
    k, n = w.shape
    w = f64(bf(w)).reshape(k // 32, 32, n)
    amax = np.abs(w).max(1)
    if fmt == "e4m3":
        byte = np.frexp(amax)[1] - 1 + 127 - 7
    else:
        mant, ex = np.frexp(amax / 6.0)
        byte = np.where(mant > 0.5, ex, ex - 1) + 127
    byte = np.clip(np.where(amax > 0, byte, 1), 1, 254)
    scaled = (w * np.exp2(127.0 - byte)[:, None, :]).reshape(k, n).astype(np.float32)
    by_word = np.ascontiguousarray(scaled.reshape(k // 512, 128, 4, n).transpose(0, 1, 3, 2))
    if fmt == "e4m3":
        words = by_word.astype(ml_dtypes.float8_e4m3fn).view(np.uint8)
    else:
        c = by_word.astype(ml_dtypes.float4_e2m1fn).view(np.uint8) & 0xF
        words = c[..., 0::2] | (c[..., 1::2] << 4)
    return np.ascontiguousarray(words), np.ascontiguousarray(byte.astype(np.uint8).reshape(k // 512, 16, n))


def unpack_weight(words, scales, fmt):
    g, p, n, _ = words.shape
    if fmt == "e4m3":
        vals = np.ascontiguousarray(words).view(ml_dtypes.float8_e4m3fn).astype(np.float64)
    else:
        nib = np.empty((g, p, n, 4), np.uint8)
        nib[..., 0::2] = words & 0xF
        nib[..., 1::2] = words >> 4
        vals = E2M1[nib]
    vals = vals * np.repeat(np.exp2(scales.astype(np.float64) - 127.0), 8, axis=1)[..., None]
    return vals.transpose(0, 1, 3, 2).reshape(g * 512, n)
def pack4(w):
    words, scales = pack_weight(w, "e2m1")
    return words.reshape(words.shape[0], 128, -1), scales


def unpack4(words, scales):
    return unpack_weight(words.reshape(words.shape[0], 128, -1, 2), scales, "e2m1")


E4M3FN = np.array([(-1.0 if i & 128 else 1.0) * ((1.0 + (i & 7) / 8.0) * 2.0 ** (((i >> 3) & 15) - 7) if i & 120 else (i & 7) * 2.0 ** -9) for i in range(256)])


def e4m3fn_bytes(y):
    return np.clip(np.asarray(y, np.float64), -448.0, 448.0).astype(np.float32).astype(ml_dtypes.float8_e4m3fn).view(np.uint8)


def e4m3fn_values(b):
    return E4M3FN[b]


T, M, N, L = 1024, 1024, 2048, 512


def log_error(e, c):
    return c[None, :] * np.sign(e) * np.log(1.0 + np.abs(e))


def proportionate_gain(w):
    aw = np.abs(w)
    mw = np.sum(aw, axis=0) * (1.0 / w.shape[0])
    return 0.5 + 0.5 * aw / (mw[None, :] + 0.001)


def draw0():
    a = mx_kscale(M)
    u = mx_kscale(T)
    x = bf(np.random.standard_normal((T, N)) / u[:, None])
    e = bf(np.random.standard_normal((T, M)) * 2.0)
    c = bf((1.0 + 0.1 * np.random.standard_normal(M)) * a)
    s_words, s_scales = pack4(np.random.standard_normal((M, L)) * (0.3 / np.sqrt(M)) / a[:, None])
    return {
        "x": x,
        "e": e,
        "c": c,
        "s_words": s_words,
        "s_scales": s_scales,
        "g": bf((1.0 + 0.1 * np.random.standard_normal(T)) * u),
        "w": bf(np.random.standard_normal((N, L)) * 0.04),
    }


def core(x, e, c, s_words, s_scales, g, w):
    x, e, c, g, w = f64(x), f64(e), f64(c), f64(g), f64(w)
    steps = x.shape[0]
    v = log_error(e, c)
    f = mxq(v, 1, "e4m3") @ unpack4(s_words, s_scales)
    fg = g[:, None] * f
    p = (1.0 / np.sqrt(steps)) * (mxq(x, 0, "e4m3").T @ mxq(fg, 0, "e4m3"))
    k = proportionate_gain(w)
    w_new = 0.9 * w + 0.5 * k * p
    return w_new


def setup_inputs():
    drawn = draw0()
    full = np.asarray(drawn['x']).astype(np.float64)
    scale = (np.abs(full).reshape(1024, 16, 128).max(axis=(2,)) / 448.0).astype(np.float32)
    given = {}
    for key, value in drawn.items():
        if key == 'x':
            given['x_bytes'] = e4m3fn_bytes(full / np.repeat(scale.astype(np.float64), 128, axis=1))
            given['x_scale'] = scale
        else:
            given[key] = value
    return given


def reference(x_bytes, x_scale, e, c, s_words, s_scales, g, w):
    return core(e4m3fn_values(x_bytes) * np.repeat(x_scale.astype(np.float64), 128, axis=1), e, c, s_words, s_scales, g, w)

@@ -1,0 +1,462 @@
+from contextlib import ExitStack
+
+import concourse.mybir as mybir
+from concourse.masks import make_identity
+
+T, M, N, L = 1024, 1024, 2048, 512
+FLOPS = 2 * T * M * L + 2 * T * N * L
+
+F32 = mybir.dt.float32
+BF16 = mybir.dt.bfloat16
+I32 = mybir.dt.int32
+U32 = mybir.dt.uint32
+U8 = mybir.dt.uint8
+FP8 = mybir.dt.float8_e4m3fn
+FP8X4 = mybir.dt.float8_e4m3fn_x4
+FP4X4 = mybir.dt.float4_e2m1fn_x4
+ALU = mybir.AluOpType
+ACT = mybir.ActivationFunctionType
+
+P = 128
+PACK = 4
+K_PASS = P * PACK
+T_PASSES = T // K_PASS
+M_PASSES = M // K_PASS
+TOKEN_TILES = T // P
+L_TILES = L // P
+N_TILES = N // P
+CHUNK = 512
+CHUNKS = N // CHUNK
+BLOCK = 128
+HALF = N // 2
+LAST = CHUNKS - 1
+
+ABS_MASK = 0x7FFF7FFF
+SIGN_MASK = 0x80008000 - (1 << 32)
+LEAK = 0.9
+GAIN = 0.25 / 32.0 / LEAK
+
+
+def tile_proportionateleakyadjointloglmsupdate_d1p_kernel(
+    tc, x_bytes, x_scale, e, c, s_words, s_scales, g, w, out
+):
+    nc = tc.nc
+    with ExitStack() as ctx:
+        keep = ctx.enter_context(tc.tile_pool(name="keep", bufs=1))
+        flow = ctx.enter_context(tc.tile_pool(name="flow", bufs=3))
+        psum = ctx.enter_context(tc.psum_pool(name="psum", bufs=1))
+        ctx.enter_context(tc.manual_schedule())
+
+        def bank(index, shape, dtype, name):
+            return psum.tile(shape, dtype, name=name, tag="bank%d" % index)
+
+        ident_f32 = keep.tile([P, P], F32, name="ident_f32")
+        ident_bf16 = keep.tile([P, P], BF16, name="ident_bf16")
+        make_identity(nc, ident_f32[:])
+        make_identity(nc, ident_bf16[:])
+        ones = keep.tile([P, 2], BF16, name="ones")
+        nc.vector.memset(ones[:], 1.0)
+        s_scale_sb = keep.tile([P, M_PASSES, L], U8, name="s_scale_sb", align_bytes=64)
+        nc.vector.memset(s_scale_sb[:].rearrange("p g n -> p (g n)").bitcast(I32), 0)
+        warm = keep.tile([P, 1], F32, name="warm")
+        nc.scalar.activation(out=warm[:], in_=ones[:, 0:1], func=ACT.Ln)
+
+        c_words = keep.tile([P, 4], F32, name="c_words")
+        nc.sync.dma_start(out=c_words[:].bitcast(BF16), in_=c.rearrange("(p i) -> p i", p=P))
+        e_rows = e.rearrange("(g p j) m -> g j p m", p=P, j=PACK)
+        e_sb = [keep.tile([P, M], BF16, name="e_sb%d" % i) for i in range(TOKEN_TILES)]
+        x_rows = x_bytes.rearrange("(g p j) n -> g p j n", p=P, j=PACK)
+        x_raw = {}
+        for h in range(2):
+            for gt in range(T_PASSES):
+                x_raw[h, gt] = keep.tile([P, PACK, HALF], U8, name="x_raw%d%d" % (h, gt))
+        xs_sb = keep.tile([P, T_PASSES, PACK * 16], F32, name="xs_sb")
+        s_sb = keep.tile([P, M_PASSES, 2 * L], U8, name="s_sb", align_bytes=64)
+        g_sb = keep.tile([P, T_PASSES, PACK], BF16, name="g_sb")
+        w_rows = w.rearrange("(c q p) l -> c p q l", p=P, q=CHUNK // P)
+        w_sb = [keep.tile([P, CHUNK // P, L], BF16, name="w_sb%d" % i) for i in range(CHUNKS)]
+
+        def load_e(i):
+            nc.sync.dma_start(out=e_sb[i][:], in_=e_rows[i // PACK, i % PACK])
+
+        def load_x(h, gt):
+            nc.sync.dma_start(out=x_raw[h, gt][:], in_=x_rows[gt][:, :, h * HALF : (h + 1) * HALF])
+
+        def load_w(ch):
+            nc.sync.dma_start(out=w_sb[ch][:], in_=w_rows[ch])
+
+        load_e(0)
+        load_e(1)
+        nc.sync.dma_start(out=xs_sb[:], in_=x_scale.rearrange("(g p j) b -> p g (j b)", p=P, j=PACK))
+        load_e(2)
+        load_x(0, 0)
+        load_e(3)
+        load_w(0)
+        load_e(4)
+        load_x(0, 1)
+        load_e(5)
+        load_w(1)
+        nc.sync.dma_start(out=s_sb[:].bitcast(I32), in_=s_words.rearrange("g p n -> p g n").bitcast(I32))
+        for q in range(4):
+            nc.sync.dma_start(
+                out=s_scale_sb[32 * q : 32 * q + 4, :, :].bitcast(I32),
+                in_=s_scales[:, 4 * q : 4 * q + 4, :].rearrange("g r n -> r g n").bitcast(I32),
+            )
+        nc.sync.dma_start(out=g_sb[:], in_=g.rearrange("(g p j) -> p g j", p=P, j=PACK))
+        load_e(6)
+        load_w(2)
+        load_e(7)
+        load_w(3)
+        load_x(1, 0)
+        load_x(1, 1)
+
+        c_bank = bank(6, [P, 4, P], F32, "c_bank")
+        for i in range(4):
+            nc.tensor.transpose(c_bank[:, i, :], c_words[:, i : i + 1].to_broadcast([P, P]), ident_f32[:])
+        c_all = keep.tile([P, 2, P, 2], F32, name="c_all")
+        nc.scalar.copy(out=c_all[:], in_=c_bank[:].rearrange("p (h u) r -> p u r h", u=2))
+
+        abs_e, signed_c, abs_bank, sc_bank, log_e, v_bf, v_codes, v_scales = {}, {}, {}, {}, {}, {}, {}, {}
+
+        def e_words(i):
+            return e_sb[i][:].bitcast(I32).rearrange("p (q u) -> p u q", u=2)
+
+        def abs_of_e(i):
+            abs_e[i] = flow.tile([P, 2, M // 4], I32, name="abs_e")
+            nc.vector.tensor_scalar(out=abs_e[i][:], in0=e_words(i), scalar1=ABS_MASK, scalar2=None, op0=ALU.bitwise_and)
+
+        def sign_of_e(i):
+            signed_c[i] = flow.tile([P, 2, M // 4], I32, name="signed_c")
+            nc.vector.scalar_tensor_tensor(
+                out=signed_c[i][:],
+                in0=e_words(i),
+                scalar=SIGN_MASK,
+                in1=c_all[:].rearrange("p u r h -> p u (r h)").bitcast(I32),
+                op0=ALU.bitwise_and,
+                op1=ALU.bitwise_xor,
+            )
+
+        def turn(src, dst):
+            words = src[:].rearrange("p u q -> p (u q)").bitcast(F32)
+            for b in range(4):
+                nc.tensor.transpose(dst[:, b, :], words[:, b * P : (b + 1) * P], ident_f32[:])
+
+        def turn_abs(i):
+            abs_bank[i] = bank(i % 2, [P, 4, P], F32, "abs_bank")
+            turn(abs_e[i], abs_bank[i])
+
+        def turn_sign(i):
+            sc_bank[i] = bank(2 + i % 2, [P, 4, P], F32, "sc_bank")
+            turn(signed_c[i], sc_bank[i])
+
+        def as_values(turned):
+            return turned[:].rearrange("p b r -> p (b r)").bitcast(BF16).rearrange("p (u r e) -> p r u e", u=2, e=2)
+
+        def log_of_abs(i):
+            log_e[i] = flow.tile([P, M], F32, name="log_e", bufs=2)
+            nc.scalar.activation(
+                out=log_e[i][:].rearrange("p (r u e) -> p r u e", u=2, e=2),
+                in_=as_values(abs_bank[i]), func=ACT.Ln, bias=1.0,
+            )
+
+        def make_v(i):
+            v_bf[i] = flow.tile([P, M], BF16, name="v_bf", align_bytes=64)
+            nc.vector.tensor_tensor(
+                out=v_bf[i][:].rearrange("p (r u e) -> p r u e", u=2, e=2),
+                in0=log_e[i][:].rearrange("p (r u e) -> p r u e", u=2, e=2),
+                in1=as_values(sc_bank[i]), op=ALU.mult,
+            )
+
+        def quantize_v(i):
+            v_codes[i] = keep.tile([P, M // PACK], U32, name="v_codes%d" % i, align_bytes=64)
+            v_scales[i] = keep.tile([P, M // PACK], U8, name="v_scales%d" % i, align_bytes=64)
+            nc.vector.quantize_mx(out=v_codes[i][:].bitcast(FP8X4), scales=v_scales[i][:], in_=v_bf[i][:])
+
+        f_bank, fg_bf, fg_codes, fg_scales = {}, {}, {}, {}
+
+        def first_matmul(gt, lt):
+            f_bank[gt, lt] = bank(4 + lt % 2, [P, PACK, P], F32, "f_bank")
+            for j in range(PACK):
+                i = gt * PACK + j
+                for gm in range(M_PASSES):
+                    nc.tensor.matmul_mx(
+                        out=f_bank[gt, lt][:, j, :],
+                        lhsT=v_codes[i][:, gm * P : (gm + 1) * P].bitcast(FP8X4),
+                        lhsT_scale=v_scales[i][:, gm * P : (gm + 1) * P],
+                        rhs=s_sb[:, gm, 2 * lt * P : 2 * (lt + 1) * P].bitcast(FP4X4),
+                        rhs_scale=s_scale_sb[:, gm, lt * P : (lt + 1) * P],
+                        start=(gm == 0),
+                        stop=(gm == M_PASSES - 1),
+                    )
+
+        def make_fg(gt, lt):
+            if lt == 0:
+                fg_bf[gt] = keep.tile([P, L, PACK], BF16, name="fg_bf%d" % gt, align_bytes=64)
+            nc.vector.tensor_tensor(
+                out=fg_bf[gt][:, lt * P : (lt + 1) * P, :],
+                in0=f_bank[gt, lt][:].rearrange("p j l -> p l j"),
+                in1=g_sb[:, gt, :].unsqueeze(1).to_broadcast([P, P, PACK]),
+                op=ALU.mult,
+            )
+
+        def quantize_fg(gt):
+            fg_codes[gt] = keep.tile([P, L], U32, name="fg_codes%d" % gt, align_bytes=64)
+            fg_scales[gt] = keep.tile([P, L], U8, name="fg_scales%d" % gt, align_bytes=64)
+            nc.vector.quantize_mx(
+                out=fg_codes[gt][:].bitcast(FP8X4), scales=fg_scales[gt][:],
+                in_=fg_bf[gt][:].rearrange("p l j -> p (l j)"),
+            )
+
+        x_wide, x_mixed, x_codes, x_scales = {}, {}, {}, {}
+
+        def widen_x(ch, gt, j):
+            if j == 0:
+                x_wide[ch, gt] = keep.tile([P, PACK, CHUNK], BF16, name="x_wide%d%d" % (ch, gt))
+            h, first = divmod(ch * CHUNK, HALF)
+            for b in range(CHUNK // BLOCK):
+                col = j * 16 + ch * (CHUNK // BLOCK) + b
+                nc.scalar.activation(
+                    out=x_wide[ch, gt][:, j, b * BLOCK : (b + 1) * BLOCK],
+                    in_=x_raw[h, gt][:, j, first + b * BLOCK : first + (b + 1) * BLOCK].bitcast(FP8),
+                    func=ACT.Copy,
+                    scale=xs_sb[:, gt, col : col + 1],
+                )
+
+        def part_cols(ch, part):
+            width = CHUNK if ch < LAST else CHUNK // 2
+            return slice(part * width, (part + 1) * width)
+
+        def mix_x(ch, gt, part):
+            cols = part_cols(ch, part)
+            x_mixed[ch, gt, part] = flow.tile([P, cols.stop - cols.start, PACK], BF16, name="x_mixed", align_bytes=64)
+            nc.vector.tensor_copy(out=x_mixed[ch, gt, part][:], in_=x_wide[ch, gt][:, :, cols].rearrange("p j n -> p n j"))
+
+        def quantize_x(ch, gt, part):
+            if part == 0:
+                x_codes[ch, gt] = keep.tile([P, CHUNK], U32, name="x_codes%d%d" % (ch, gt), align_bytes=64)
+                x_scales[ch, gt] = keep.tile([P, CHUNK], U8, name="x_scales%d%d" % (ch, gt), align_bytes=64)
+            cols = part_cols(ch, part)
+            nc.vector.quantize_mx(
+                out=x_codes[ch, gt][:, cols].bitcast(FP8X4), scales=x_scales[ch, gt][:, cols],
+                in_=x_mixed[ch, gt, part][:].rearrange("p n j -> p (n j)"),
+            )
+
+        abs_w = {}
+
+        def abs_of_w(ch):
+            abs_w[ch] = flow.tile([P, CHUNK // P, L], BF16, name="abs_w", bufs=2)
+            nc.vector.tensor_scalar(
+                out=abs_w[ch][:].bitcast(I32), in0=w_sb[ch][:].bitcast(I32),
+                scalar1=ABS_MASK, scalar2=None, op0=ALU.bitwise_and,
+            )
+
+        gain_scale = keep.tile([P, L_TILES], F32, name="gain_scale")
+
+        sums = {}
+
+        def column_sums(ch):
+            if ch == 0:
+                sums[0] = bank(6, [P, L_TILES, CHUNKS, 2], F32, "sums")
+            for lt in range(L_TILES):
+                for q in range(CHUNK // P):
+                    nc.tensor.matmul(
+                        out=sums[0][:, lt, ch, :],
+                        lhsT=abs_w[ch][:, q, lt * P : (lt + 1) * P],
+                        rhs=ones[:],
+                        start=(q == 0),
+                        stop=(q == CHUNK // P - 1),
+                    )
+
+        total = keep.tile([P, L_TILES], F32, name="total")
+        denom = keep.tile([P, L_TILES], F32, name="denom")
+
+        def add_sums():
+            nc.vector.tensor_reduce(out=total[:], in_=sums[0][:, :, :, 0], axis=mybir.AxisListType.X, op=ALU.add)
+
+        def make_denom():
+            nc.vector.tensor_scalar(
+                out=denom[:], in0=total[:], scalar1=1.0 / (N * GAIN), scalar2=0.001 / GAIN,
+                op0=ALU.mult, op1=ALU.add,
+            )
+
+        def invert_denom():
+            nc.vector.reciprocal(out=gain_scale[:], in_=denom[:])
+
+        w_bank, gain, acc, update, out_bank = {}, {}, {}, {}, {}
+
+        def turn_w(h, lt):
+            w_bank[h, lt] = bank(6 + lt % 2, [P, HALF], BF16, "w_bank")
+            for i in range(HALF // P):
+                nc.tensor.transpose(
+                    w_bank[h, lt][:, i * P : (i + 1) * P],
+                    w_sb[2 * h + i // 4][:, i % 4, lt * P : (lt + 1) * P],
+                    ident_bf16[:],
+                )
+
+        def make_gain(h, lt):
+            if lt == 0:
+                gain[h] = keep.tile([P, L_TILES, HALF], F32, name="gain%d" % h)
+            nc.scalar.activation(out=gain[h][:, lt, :], in_=w_bank[h, lt][:], func=ACT.Abs, scale=gain_scale[:, lt : lt + 1])
+
+        def second_matmul(ch, k):
+            acc[ch, k] = bank(k, [P, CHUNK], F32, "acc")
+            if ch < LAST:
+                groups = [(k, acc[ch, k][:], slice(0, CHUNK))]
+            else:
+                groups = [(lt, acc[ch, k][:, lt * P : (lt + 1) * P], slice(k * P, (k + 1) * P)) for lt in range(L_TILES)]
+            for lt, dst, cols in groups:
+                for gt in range(T_PASSES):
+                    nc.tensor.matmul_mx(
+                        out=dst,
+                        lhsT=fg_codes[gt][:, lt * P : (lt + 1) * P].bitcast(FP8X4),
+                        lhsT_scale=fg_scales[gt][:, lt * P : (lt + 1) * P],
+                        rhs=x_codes[ch, gt][:, cols].bitcast(FP8X4),
+                        rhs_scale=x_scales[ch, gt][:, cols],
+                        start=(gt == 0),
+                        stop=(gt == T_PASSES - 1),
+                    )
+
+        def make_update(ch, k):
+            update[ch, k] = flow.tile([P, CHUNK], F32, name="update", tag="update%d" % (ch % 2 * 4 + k), bufs=1)
+            h, first = divmod(ch * CHUNK, HALF)
+            if ch < LAST:
+                dst, factor, product = update[ch, k][:], gain[h][:, k, first : first + CHUNK], acc[ch, k][:]
+            else:
+                dst = update[ch, k][:].rearrange("p (t n) -> p t n", t=L_TILES)
+                factor = gain[h][:, :, first + k * P : first + (k + 1) * P]
+                product = acc[ch, k][:].rearrange("p (t n) -> p t n", t=L_TILES)
+            nc.vector.scalar_tensor_tensor(out=dst, in0=factor, scalar=GAIN, in1=product, op0=ALU.add, op1=ALU.mult)
+
+        def turn_back(ch, q):
+            out_bank[ch, q] = bank(4 + q, [P, L], F32, "out_bank")
+            nc.tensor.matmul(out=out_bank[ch, q][:], lhsT=ident_bf16[:], rhs=w_sb[ch][:, q, :], start=True, stop=False)
+            for lt in range(L_TILES):
+                nc.tensor.matmul(
+                    out=out_bank[ch, q][:, lt * P : (lt + 1) * P],
+                    lhsT=update[ch, lt][:, q * P : (q + 1) * P] if ch < LAST else update[ch, q][:, lt * P : (lt + 1) * P],
+                    rhs=ident_f32[:],
+                    is_transpose=True,
+                    start=False,
+                    stop=(lt == L_TILES - 1),
+                )
+
+        def store(ch, q):
+            result = flow.tile([P, L], F32, name="result", bufs=6)
+            nc.scalar.activation(out=result[:], in_=out_bank[ch, q][:], func=ACT.Copy, scale=LEAK)
+            row = ch * CHUNK + q * P
+            nc.sync.dma_start(out=out[row : row + P, :], in_=result[:])
+
+        quad = range(4)
+
+        def needs(step):
+            fn, a = step[0], step[1:]
+            if fn is turn_abs:
+                return [(abs_of_e,) + a, (log_of_abs, a[0] - 2)]
+            if fn is turn_sign:
+                return [(sign_of_e,) + a, (make_v, a[0] - 2)]
+            if fn is abs_of_e:
+                return [(turn_abs, a[0] - 3)]
+            if fn is sign_of_e:
+                return [(turn_sign, a[0] - 3)]
+            if fn is log_of_abs:
+                return [(turn_abs,) + a, (make_v, a[0] - 2)]
+            if fn is make_v:
+                return [(log_of_abs,) + a, (turn_sign,) + a]
+            if fn is first_matmul:
+                before = a[0] * L_TILES + a[1] - 2
+                return [(quantize_v, a[0] * PACK + j) for j in quad] + [(make_fg, before // L_TILES, before % L_TILES)]
+            if fn is make_fg:
+                return [(first_matmul,) + a]
+            if fn is mix_x:
+                return [(widen_x,) + a[:2] + (j,) for j in quad]
+            if fn is abs_of_w:
+                return [(column_sums, a[0] - 2)]
+            if fn is column_sums:
+                return [(abs_of_w,) + a]
+            if fn is add_sums:
+                return [(column_sums, ch) for ch in quad]
+            if fn is turn_w:
+                before = a[0] * L_TILES + a[1] - 2
+                return [(add_sums,), (make_gain, before // L_TILES, before % L_TILES)]
+            if fn is make_gain:
+                return [(turn_w,) + a, (invert_denom,)]
+            if fn is second_matmul:
+                part = a[1] // 2 if a[0] == LAST else 0
+                return [(quantize_x, a[0], 0, part), (quantize_x, a[0], 1, part), (quantize_fg, 0), (quantize_fg, 1),
+                        (make_update, a[0] - 1, a[1]), (make_v, TOKEN_TILES - 1)]
+            if fn is make_update:
+                return [(second_matmul,) + a] + [(make_gain, a[0] // 2, lt) for lt in quad] + [(turn_back, a[0] - 2, q) for q in quad]
+            if fn is turn_back:
+                return [(make_update, a[0], lt) for lt in (quad if a[0] < LAST else [a[1]])] + [(store, a[0] - 1, a[1]), (make_gain, 1, 2), (make_gain, 1, 3), (make_fg, 1, 3)]
+            if fn is store:
+                return [(turn_back,) + a]
+            return []
+
+        vector = [(abs_of_e, 0), (abs_of_e, 1), (sign_of_e, 0)]
+        for i in range(TOKEN_TILES):
+            vector += [(abs_of_e, i + 2), (sign_of_e, i + 1), (abs_of_w, i - 2), (make_v, i), (quantize_v, i - 1)]
+            if i == 6:
+                vector += [(add_sums,), (make_fg, 0, 1), (make_denom,)]
+            elif i == 7:
+                vector.insert(-2, (invert_denom,))
+                vector += [(make_fg, 0, 2)]
+            else:
+                vector += [(make_fg, 0, i - 5)]
+        vector += [(quantize_v, 7), (make_fg, 0, 3), (mix_x, 0, 0, 0), (quantize_fg, 0)]
+        vector += [(make_fg, 1, 0), (make_fg, 1, 1), (mix_x, 0, 1, 0), (make_fg, 1, 2), (make_fg, 1, 3)]
+        vector += [(quantize_x, 0, 0, 0), (quantize_fg, 1), (quantize_x, 0, 1, 0)]
+        for ch in range(2):
+            vector += [(mix_x, ch + 1, 0, 0)] + [(make_update, ch, k) for k in quad]
+            vector += [(mix_x, ch + 1, 1, 0), (quantize_x, ch + 1, 0, 0), (quantize_x, ch + 1, 1, 0)]
+        vector += [(mix_x, 3, 0, 0)] + [(make_update, 2, k) for k in quad] + [(mix_x, 3, 1, 0)]
+        vector += [(quantize_x, 3, 0, 0), (quantize_x, 3, 1, 0), (mix_x, 3, 0, 1), (mix_x, 3, 1, 1)]
+        vector += [(quantize_x, 3, 0, 1), (quantize_x, 3, 1, 1)] + [(make_update, 3, k) for k in quad]
+
+        def widen(ch, gt, js=quad):
+            return [(widen_x, ch, gt, j) for j in js]
+
+        def stores(ch):
+            return [(store, ch, q) for q in quad]
+
+        planes = [step for ch in range(CHUNKS) for gt in range(T_PASSES) for step in widen(ch, gt)]
+        gains = [(make_gain, h, lt) for h in range(2) for lt in quad]
+        scalar = [(log_of_abs, 0)]
+        for i in range(TOKEN_TILES):
+            scalar += [(log_of_abs, i + 1)] + planes[2 * i : 2 * i + 2]
+        for k in range(8):
+            scalar += [planes[16 + k], gains[k]]
+        scalar += planes[24:26] + stores(0) + planes[26:32] + stores(1) + stores(2) + stores(3)
+
+        turns = [(turn_w, h, lt) for h in range(2) for lt in quad]
+
+        def seconds(ch):
+            return [(second_matmul, ch, k) for k in quad]
+
+        def backs(ch):
+            return [(turn_back, ch, q) for q in quad]
+
+        tensor = [(turn_abs, 0), (turn_abs, 1), (turn_sign, 0)]
+        for i in range(TOKEN_TILES):
+            tensor += [(turn_abs, i + 2), (turn_sign, i + 1), (column_sums, i - 2), (first_matmul, 0, i - 4)]
+        tensor.insert(-1, turns[0])
+        tensor += turns[1:2] + [(first_matmul, 1, 0), (first_matmul, 1, 1)] + turns[2:4]
+        tensor += [(first_matmul, 1, 2), (first_matmul, 1, 3)] + turns[4:6]
+        tensor += seconds(0)[:2] + turns[6:7] + seconds(0)[2:] + turns[7:8] + backs(0) + seconds(1) + backs(1) + seconds(2)
+        tensor += backs(2)[:2] + seconds(3)[:2] + backs(2)[2:] + seconds(3)[2:] + backs(3)
+
+        limits = {abs_of_e: 8, sign_of_e: 8, make_v: 8, quantize_v: 8, log_of_abs: 8, turn_abs: 8, turn_sign: 8}
+
+        def real(step):
+            return all(0 <= k < limits.get(step[0], 4) for k in step[1:])
+
+        queues = [[step for step in queue if real(step)] for queue in (vector, scalar, tensor)]
+        done = set()
+        while any(queues):
+            moved = False
+            for queue in queues:
+                while queue and all(n in done or not real(n) for n in needs(queue[0])):
+                    step = queue.pop(0)
+                    step[0](*step[1:])
+                    done.add(step)
+                    moved = True
+            assert moved

@@ -29,7 +29,11 @@ CHUNK = 512
 CHUNKS = N // CHUNK
 BLOCK = 128
 HALF = N // 2
-LAST = CHUNKS - 1
+STRIP = 256
+WL = 4
+WIDE_FROM = 4
+ON_SCALAR = [(7, 0), (7, 1)]
+STRIPS = N // STRIP
 
 ABS_MASK = 0x7FFF7FFF
 SIGN_MASK = 0x80008000 - (1 << 32)
@@ -91,11 +95,11 @@ def tile_proportionateleakyadjointloglmsupdate_d1p_kernel(
         load_e(2)
         load_x(0, 0)
         load_e(3)
-        load_w(0)
         load_e(4)
         load_x(0, 1)
         load_e(5)
-        load_w(1)
+        load_e(6)
+        load_e(7)
         nc.sync.dma_start(out=s_sb[:].bitcast(I32), in_=s_words.rearrange("g p n -> p g n").bitcast(I32))
         for q in range(4):
             nc.sync.dma_start(
@@ -103,10 +107,8 @@ def tile_proportionateleakyadjointloglmsupdate_d1p_kernel(
                 in_=s_scales[:, 4 * q : 4 * q + 4, :].rearrange("g r n -> r g n").bitcast(I32),
             )
         nc.sync.dma_start(out=g_sb[:], in_=g.rearrange("(g p j) -> p g j", p=P, j=PACK))
-        load_e(6)
-        load_w(2)
-        load_e(7)
-        load_w(3)
+        for ch in range(CHUNKS):
+            load_w(ch)
         load_x(1, 0)
         load_x(1, 1)
 
@@ -193,9 +195,9 @@ def tile_proportionateleakyadjointloglmsupdate_d1p_kernel(
             if lt == 0:
                 fg_bf[gt] = keep.tile([P, L, PACK], BF16, name="fg_bf%d" % gt, align_bytes=64)
             nc.vector.tensor_tensor(
-                out=fg_bf[gt][:, lt * P : (lt + 1) * P, :],
-                in0=f_bank[gt, lt][:].rearrange("p j l -> p l j"),
-                in1=g_sb[:, gt, :].unsqueeze(1).to_broadcast([P, P, PACK]),
+                out=fg_bf[gt][:, lt * P : (lt + 1) * P, :].rearrange("p (c i) j -> p c j i", i=4),
+                in0=f_bank[gt, lt][:].rearrange("p j (c i) -> p c j i", i=4),
+                in1=g_sb[:, gt, :].unsqueeze(1).unsqueeze(3).to_broadcast([P, P // 4, PACK, 4]),
                 op=ALU.mult,
             )
 
@@ -209,36 +211,35 @@ def tile_proportionateleakyadjointloglmsupdate_d1p_kernel(
 
         x_wide, x_mixed, x_codes, x_scales = {}, {}, {}, {}
 
-        def widen_x(ch, gt, j):
-            if j == 0:
-                x_wide[ch, gt] = keep.tile([P, PACK, CHUNK], BF16, name="x_wide%d%d" % (ch, gt))
-            h, first = divmod(ch * CHUNK, HALF)
-            for b in range(CHUNK // BLOCK):
-                col = j * 16 + ch * (CHUNK // BLOCK) + b
-                nc.scalar.activation(
-                    out=x_wide[ch, gt][:, j, b * BLOCK : (b + 1) * BLOCK],
-                    in_=x_raw[h, gt][:, j, first + b * BLOCK : first + (b + 1) * BLOCK].bitcast(FP8),
-                    func=ACT.Copy,
-                    scale=xs_sb[:, gt, col : col + 1],
-                )
+        def widen_x(st, gt):
+            x_wide[st, gt] = keep.tile([P, PACK, STRIP], BF16, name="x_wide%d%d" % (st, gt))
+            h, first = divmod(st * STRIP, HALF)
+            for j in range(PACK):
+                for b in range(STRIP // BLOCK):
+                    col = j * (N // BLOCK) + st * (STRIP // BLOCK) + b
+                    nc.scalar.activation(
+                        out=x_wide[st, gt][:, j, b * BLOCK : (b + 1) * BLOCK],
+                        in_=x_raw[h, gt][:, j, first + b * BLOCK : first + (b + 1) * BLOCK].bitcast(FP8),
+                        func=ACT.Copy,
+                        scale=xs_sb[:, gt, col : col + 1],
+                    )
 
-        def part_cols(ch, part):
-            width = CHUNK if ch < LAST else CHUNK // 2
-            return slice(part * width, (part + 1) * width)
+        def mix_x(st, gt):
+            if gt == 0:
+                x_mixed[st] = flow.tile([P, T_PASSES, STRIP, PACK], BF16, name="x_mixed", align_bytes=64, bufs=3)
+            copy = nc.scalar.copy if (st, gt) in ON_SCALAR else nc.vector.tensor_copy
+            copy(
+                out=x_mixed[st][:, gt].rearrange("p (c i) j -> p c j i", i=4),
+                in_=x_wide[st, gt][:].rearrange("p j (c i) -> p c j i", i=4),
+            )
 
-        def mix_x(ch, gt, part):
-            cols = part_cols(ch, part)
-            x_mixed[ch, gt, part] = flow.tile([P, cols.stop - cols.start, PACK], BF16, name="x_mixed", align_bytes=64)
-            nc.vector.tensor_copy(out=x_mixed[ch, gt, part][:], in_=x_wide[ch, gt][:, :, cols].rearrange("p j n -> p n j"))
-
-        def quantize_x(ch, gt, part):
-            if part == 0:
-                x_codes[ch, gt] = keep.tile([P, CHUNK], U32, name="x_codes%d%d" % (ch, gt), align_bytes=64)
-                x_scales[ch, gt] = keep.tile([P, CHUNK], U8, name="x_scales%d%d" % (ch, gt), align_bytes=64)
-            cols = part_cols(ch, part)
+        def quantize_x(st):
+            x_codes[st] = keep.tile([P, T_PASSES, STRIP], U32, name="x_codes%d" % st, align_bytes=64)
+            x_scales[st] = keep.tile([P, T_PASSES, STRIP], U8, name="x_scales%d" % st, align_bytes=64)
             nc.vector.quantize_mx(
-                out=x_codes[ch, gt][:, cols].bitcast(FP8X4), scales=x_scales[ch, gt][:, cols],
-                in_=x_mixed[ch, gt, part][:].rearrange("p n j -> p (n j)"),
+                out=x_codes[st][:].rearrange("p g n -> p (g n)").bitcast(FP8X4),
+                scales=x_scales[st][:].rearrange("p g n -> p (g n)"),
+                in_=x_mixed[st][:].rearrange("p g n j -> p (g n j)"),
             )
 
         abs_w = {}
@@ -298,55 +299,50 @@ def tile_proportionateleakyadjointloglmsupdate_d1p_kernel(
                 gain[h] = keep.tile([P, L_TILES, HALF], F32, name="gain%d" % h)
             nc.scalar.activation(out=gain[h][:, lt, :], in_=w_bank[h, lt][:], func=ACT.Abs, scale=gain_scale[:, lt : lt + 1])
 
-        def second_matmul(ch, k):
-            acc[ch, k] = bank(k, [P, CHUNK], F32, "acc")
-            if ch < LAST:
-                groups = [(k, acc[ch, k][:], slice(0, CHUNK))]
-            else:
-                groups = [(lt, acc[ch, k][:, lt * P : (lt + 1) * P], slice(k * P, (k + 1) * P)) for lt in range(L_TILES)]
-            for lt, dst, cols in groups:
+        def second_matmul(st, k):
+            acc[st, k] = bank(st % 2 * 2 + k, [P, 2, STRIP], F32, "acc")
+            for side in range(2):
+                lt = 2 * k + side
                 for gt in range(T_PASSES):
                     nc.tensor.matmul_mx(
-                        out=dst,
+                        out=acc[st, k][:, side, :],
                         lhsT=fg_codes[gt][:, lt * P : (lt + 1) * P].bitcast(FP8X4),
                         lhsT_scale=fg_scales[gt][:, lt * P : (lt + 1) * P],
-                        rhs=x_codes[ch, gt][:, cols].bitcast(FP8X4),
-                        rhs_scale=x_scales[ch, gt][:, cols],
+                        rhs=x_codes[st][:, gt, :].bitcast(FP8X4),
+                        rhs_scale=x_scales[st][:, gt, :],
                         start=(gt == 0),
                         stop=(gt == T_PASSES - 1),
                     )
 
-        def make_update(ch, k):
-            update[ch, k] = flow.tile([P, CHUNK], F32, name="update", tag="update%d" % (ch % 2 * 4 + k), bufs=1)
-            h, first = divmod(ch * CHUNK, HALF)
-            if ch < LAST:
-                dst, factor, product = update[ch, k][:], gain[h][:, k, first : first + CHUNK], acc[ch, k][:]
-            else:
-                dst = update[ch, k][:].rearrange("p (t n) -> p t n", t=L_TILES)
-                factor = gain[h][:, :, first + k * P : first + (k + 1) * P]
-                product = acc[ch, k][:].rearrange("p (t n) -> p t n", t=L_TILES)
-            nc.vector.scalar_tensor_tensor(out=dst, in0=factor, scalar=GAIN, in1=product, op0=ALU.add, op1=ALU.mult)
+        def make_update(st, k):
+            update[st, k] = flow.tile([P, 2, STRIP], F32, name="update", bufs=6)
+            h, first = divmod(st * STRIP, HALF)
+            nc.vector.scalar_tensor_tensor(
+                out=update[st, k][:], in0=gain[h][:, 2 * k : 2 * k + 2, first : first + STRIP], scalar=GAIN,
+                in1=acc[st, k][:], op0=ALU.add, op1=ALU.mult,
+            )
 
-        def turn_back(ch, q):
-            out_bank[ch, q] = bank(4 + q, [P, L], F32, "out_bank")
-            nc.tensor.matmul(out=out_bank[ch, q][:], lhsT=ident_bf16[:], rhs=w_sb[ch][:, q, :], start=True, stop=False)
+        def turn_back(st, q):
+            i = 2 * st + q
+            out_bank[st, q] = bank(4 + (i % 4 if st >= WIDE_FROM else q), [P, L], F32, "out_bank")
+            nc.tensor.matmul(out=out_bank[st, q][:], lhsT=ident_bf16[:], rhs=w_sb[i // 4][:, i % 4, :], start=True, stop=False)
             for lt in range(L_TILES):
                 nc.tensor.matmul(
-                    out=out_bank[ch, q][:, lt * P : (lt + 1) * P],
-                    lhsT=update[ch, lt][:, q * P : (q + 1) * P] if ch < LAST else update[ch, q][:, lt * P : (lt + 1) * P],
+                    out=out_bank[st, q][:, lt * P : (lt + 1) * P],
+                    lhsT=update[st, lt // 2][:, lt % 2, q * P : (q + 1) * P],
                     rhs=ident_f32[:],
                     is_transpose=True,
                     start=False,
                     stop=(lt == L_TILES - 1),
                 )
 
-        def store(ch, q):
+        def store(st, q):
             result = flow.tile([P, L], F32, name="result", bufs=6)
-            nc.scalar.activation(out=result[:], in_=out_bank[ch, q][:], func=ACT.Copy, scale=LEAK)
-            row = ch * CHUNK + q * P
+            nc.scalar.activation(out=result[:], in_=out_bank[st, q][:], func=ACT.Copy, scale=LEAK)
+            row = st * STRIP + q * P
             nc.sync.dma_start(out=out[row : row + P, :], in_=result[:])
 
-        quad = range(4)
+        pair, quad = range(2), range(4)
 
         def needs(step):
             fn, a = step[0], step[1:]
@@ -363,12 +359,14 @@ def tile_proportionateleakyadjointloglmsupdate_d1p_kernel(
             if fn is make_v:
                 return [(log_of_abs,) + a, (turn_sign,) + a]
             if fn is first_matmul:
-                before = a[0] * L_TILES + a[1] - 2
-                return [(quantize_v, a[0] * PACK + j) for j in quad] + [(make_fg, before // L_TILES, before % L_TILES)]
+                before = divmod(a[0] * L_TILES + a[1] - 2, L_TILES)
+                return [(quantize_v, a[0] * PACK + j) for j in quad] + [(make_fg,) + before]
             if fn is make_fg:
                 return [(first_matmul,) + a]
             if fn is mix_x:
-                return [(widen_x,) + a[:2] + (j,) for j in quad]
+                return [(widen_x,) + a, (mix_x, a[0], a[1] - 1), (quantize_x, a[0] - 3)]
+            if fn is quantize_x:
+                return [(mix_x, a[0], gt) for gt in pair]
             if fn is abs_of_w:
                 return [(column_sums, a[0] - 2)]
             if fn is column_sums:
@@ -376,78 +374,61 @@ def tile_proportionateleakyadjointloglmsupdate_d1p_kernel(
             if fn is add_sums:
                 return [(column_sums, ch) for ch in quad]
             if fn is turn_w:
-                before = a[0] * L_TILES + a[1] - 2
-                return [(add_sums,), (make_gain, before // L_TILES, before % L_TILES)]
+                return [(add_sums,), (make_gain,) + divmod(a[0] * L_TILES + a[1] - 2, L_TILES)]
             if fn is make_gain:
                 return [(turn_w,) + a, (invert_denom,)]
             if fn is second_matmul:
-                part = a[1] // 2 if a[0] == LAST else 0
-                return [(quantize_x, a[0], 0, part), (quantize_x, a[0], 1, part), (quantize_fg, 0), (quantize_fg, 1),
-                        (make_update, a[0] - 1, a[1]), (make_v, TOKEN_TILES - 1)]
+                return [(quantize_x, a[0]), (quantize_fg, 0), (quantize_fg, 1), (make_update, a[0] - 2, a[1])]
             if fn is make_update:
-                return [(second_matmul,) + a] + [(make_gain, a[0] // 2, lt) for lt in quad] + [(turn_back, a[0] - 2, q) for q in quad]
+                gains = [(make_gain, a[0] * STRIP // HALF, 2 * a[1] + side) for side in pair]
+                return [(second_matmul,) + a] + gains + [(turn_back, a[0] - 3, q) for q in pair]
             if fn is turn_back:
-                return [(make_update, a[0], lt) for lt in (quad if a[0] < LAST else [a[1]])] + [(store, a[0] - 1, a[1]), (make_gain, 1, 2), (make_gain, 1, 3), (make_fg, 1, 3)]
+                free = [(make_gain, 1, 2 + a[1])] if a[0] == WIDE_FROM else [(store, a[0] - (2 if a[0] > WIDE_FROM else 1), a[1])]
+                return [(make_update, a[0], k) for k in pair] + free
             if fn is store:
                 return [(turn_back,) + a]
             return []
 
         vector = [(abs_of_e, 0), (abs_of_e, 1), (sign_of_e, 0)]
         for i in range(TOKEN_TILES):
-            vector += [(abs_of_e, i + 2), (sign_of_e, i + 1), (abs_of_w, i - 2), (make_v, i), (quantize_v, i - 1)]
-            if i == 6:
-                vector += [(add_sums,), (make_fg, 0, 1), (make_denom,)]
-            elif i == 7:
-                vector.insert(-2, (invert_denom,))
-                vector += [(make_fg, 0, 2)]
-            else:
-                vector += [(make_fg, 0, i - 5)]
-        vector += [(quantize_v, 7), (make_fg, 0, 3), (mix_x, 0, 0, 0), (quantize_fg, 0)]
-        vector += [(make_fg, 1, 0), (make_fg, 1, 1), (mix_x, 0, 1, 0), (make_fg, 1, 2), (make_fg, 1, 3)]
-        vector += [(quantize_x, 0, 0, 0), (quantize_fg, 1), (quantize_x, 0, 1, 0)]
-        for ch in range(2):
-            vector += [(mix_x, ch + 1, 0, 0)] + [(make_update, ch, k) for k in quad]
-            vector += [(mix_x, ch + 1, 1, 0), (quantize_x, ch + 1, 0, 0), (quantize_x, ch + 1, 1, 0)]
-        vector += [(mix_x, 3, 0, 0)] + [(make_update, 2, k) for k in quad] + [(mix_x, 3, 1, 0)]
-        vector += [(quantize_x, 3, 0, 0), (quantize_x, 3, 1, 0), (mix_x, 3, 0, 1), (mix_x, 3, 1, 1)]
-        vector += [(quantize_x, 3, 0, 1), (quantize_x, 3, 1, 1)] + [(make_update, 3, k) for k in quad]
+            vector += [(abs_of_e, i + 2), (sign_of_e, i + 1), (abs_of_w, i - WL), (make_v, i), (quantize_v, i - 1)]
+            vector += [(make_fg, 0, i - 5)]
+        vector += [(add_sums,), (quantize_v, 7), (make_denom,), (make_fg, 0, 3), (invert_denom,)]
+        vector += [(mix_x, 0, 0), (quantize_fg, 0), (mix_x, 0, 1), (make_fg, 1, 0), (make_fg, 1, 1), (quantize_x, 0)]
+        vector += [(mix_x, 1, 0), (make_fg, 1, 2), (make_fg, 1, 3), (mix_x, 1, 1), (quantize_fg, 1), (quantize_x, 1)]
+        vector += [(mix_x, 2, 0), (mix_x, 2, 1), (make_update, 0, 0), (quantize_x, 2), (make_update, 0, 1)]
+        vector += [(make_update, 1, 0), (make_update, 1, 1)]
+        for st in range(2, STRIPS):
+            vector += [(mix_x, st + 1, 0), (mix_x, st + 1, 1), (make_update, st, 0), (quantize_x, st + 1), (make_update, st, 1)]
 
-        def widen(ch, gt, js=quad):
-            return [(widen_x, ch, gt, j) for j in js]
+        vector = [step for step in vector if step[0] is not mix_x or step[1:] not in ON_SCALAR]
 
-        def stores(ch):
-            return [(store, ch, q) for q in quad]
-
-        planes = [step for ch in range(CHUNKS) for gt in range(T_PASSES) for step in widen(ch, gt)]
-        gains = [(make_gain, h, lt) for h in range(2) for lt in quad]
+        wides = [(widen_x, st, gt) for st in range(STRIPS) for gt in pair]
+        gains = [(make_gain, h, lt) for h in pair for lt in quad]
         scalar = [(log_of_abs, 0)]
         for i in range(TOKEN_TILES):
-            scalar += [(log_of_abs, i + 1)] + planes[2 * i : 2 * i + 2]
-        for k in range(8):
-            scalar += [planes[16 + k], gains[k]]
-        scalar += planes[24:26] + stores(0) + planes[26:32] + stores(1) + stores(2) + stores(3)
+            scalar += [(log_of_abs, i + 1), wides[i]]
+        scalar += wides[8:11] + gains[0:2] + wides[11:12] + gains[2:4] + wides[12:14]
+        extra = [gains[4:6], wides[14:16], gains[6:8], [(mix_x, 7, 0)], [(mix_x, 7, 1)], [], [], []]
+        for st in range(STRIPS):
+            scalar += extra[st] + [(store, st, q) for q in pair]
 
-        turns = [(turn_w, h, lt) for h in range(2) for lt in quad]
-
-        def seconds(ch):
-            return [(second_matmul, ch, k) for k in quad]
-
-        def backs(ch):
-            return [(turn_back, ch, q) for q in quad]
-
+        turns = [(turn_w, h, lt) for h in pair for lt in quad]
         tensor = [(turn_abs, 0), (turn_abs, 1), (turn_sign, 0)]
         for i in range(TOKEN_TILES):
-            tensor += [(turn_abs, i + 2), (turn_sign, i + 1), (column_sums, i - 2), (first_matmul, 0, i - 4)]
-        tensor.insert(-1, turns[0])
-        tensor += turns[1:2] + [(first_matmul, 1, 0), (first_matmul, 1, 1)] + turns[2:4]
-        tensor += [(first_matmul, 1, 2), (first_matmul, 1, 3)] + turns[4:6]
-        tensor += seconds(0)[:2] + turns[6:7] + seconds(0)[2:] + turns[7:8] + backs(0) + seconds(1) + backs(1) + seconds(2)
-        tensor += backs(2)[:2] + seconds(3)[:2] + backs(2)[2:] + seconds(3)[2:] + backs(3)
+            tensor += [(turn_abs, i + 2), (turn_sign, i + 1), (column_sums, i - WL), (first_matmul, 0, i - 4)]
+        tensor += turns[0:2] + [(first_matmul, 1, 0), (first_matmul, 1, 1)] + turns[2:3]
+        tensor += [(first_matmul, 1, 2), (first_matmul, 1, 3)] + turns[3:5]
+        tensor += [(second_matmul, st, k) for st in pair for k in pair] + turns[5:6]
+        tensor += [(turn_back, 0, q) for q in pair]
+        for st in range(2, STRIPS + 1):
+            tensor += [(second_matmul, st, k) for k in pair] + [(turn_back, st - 1, q) for q in pair]
+            tensor += turns[6:8] if st == 2 else []
 
-        limits = {abs_of_e: 8, sign_of_e: 8, make_v: 8, quantize_v: 8, log_of_abs: 8, turn_abs: 8, turn_sign: 8}
+        counts = {abs_of_w: CHUNKS, column_sums: CHUNKS}
 
         def real(step):
-            return all(0 <= k < limits.get(step[0], 4) for k in step[1:])
+            return all(0 <= k < counts.get(step[0], STRIPS) for k in step[1:])
 
         queues = [[step for step in queue if real(step)] for queue in (vector, scalar, tensor)]
         done = set()

@@ -31,8 +31,9 @@ BLOCK = 128
 HALF = N // 2
 STRIP = 256
 WL = 4
-WIDE_FROM = 4
-ON_SCALAR = [(7, 0), (7, 1)]
+WIDE_FROM = 1
+ON_SCALAR = [7]
+FINISH_ON_VECTOR = []
 STRIPS = N // STRIP
 
 ABS_MASK = 0x7FFF7FFF
@@ -67,39 +68,42 @@ def tile_proportionateleakyadjointloglmsupdate_d1p_kernel(
 
         c_words = keep.tile([P, 4], F32, name="c_words")
         nc.sync.dma_start(out=c_words[:].bitcast(BF16), in_=c.rearrange("(p i) -> p i", p=P))
-        e_rows = e.rearrange("(g p j) m -> g j p m", p=P, j=PACK)
-        e_sb = [keep.tile([P, M], BF16, name="e_sb%d" % i) for i in range(TOKEN_TILES)]
+        e_rows = e.rearrange("(g p j) m -> g p j m", p=P, j=PACK)
+        e_sb = [keep.tile([P, 2, M], BF16, name="e_sb%d" % i) for i in range(TOKEN_TILES // 2)]
         x_rows = x_bytes.rearrange("(g p j) n -> g p j n", p=P, j=PACK)
         x_raw = {}
-        for h in range(2):
-            for gt in range(T_PASSES):
-                x_raw[h, gt] = keep.tile([P, PACK, HALF], U8, name="x_raw%d%d" % (h, gt))
         xs_sb = keep.tile([P, T_PASSES, PACK * 16], F32, name="xs_sb")
         s_sb = keep.tile([P, M_PASSES, 2 * L], U8, name="s_sb", align_bytes=64)
         g_sb = keep.tile([P, T_PASSES, PACK], BF16, name="g_sb")
         w_rows = w.rearrange("(c q p) l -> c p q l", p=P, q=CHUNK // P)
-        w_sb = [keep.tile([P, CHUNK // P, L], BF16, name="w_sb%d" % i) for i in range(CHUNKS)]
+        w_sb = keep.tile([P, N_TILES, L], BF16, name="w_sb")
 
-        def load_e(i):
-            nc.sync.dma_start(out=e_sb[i][:], in_=e_rows[i // PACK, i % PACK])
+        def load_e(i, count):
+            gt, j = divmod(i, PACK)
+            nc.sync.dma_start(out=e_sb[i // 2][:, i % 2 : i % 2 + count, :], in_=e_rows[gt][:, j : j + count, :])
 
-        def load_x(h, gt):
-            nc.sync.dma_start(out=x_raw[h, gt][:], in_=x_rows[gt][:, :, h * HALF : (h + 1) * HALF])
+        def load_x(gt, first, last):
+            raw = keep.tile([P, PACK, (last - first) * STRIP], U8, name="x_raw%d%d" % (gt, first))
+            nc.sync.dma_start(out=raw[:], in_=x_rows[gt][:, :, first * STRIP : last * STRIP])
+            for st in range(first, last):
+                x_raw[st, gt] = raw[:, :, (st - first) * STRIP : (st - first + 1) * STRIP]
 
         def load_w(ch):
-            nc.sync.dma_start(out=w_sb[ch][:], in_=w_rows[ch])
+            nc.sync.dma_start(out=w_sb[:, 4 * ch : 4 * ch + 4, :], in_=w_rows[ch])
 
-        load_e(0)
-        load_e(1)
+        load_e(0, 1)
         nc.sync.dma_start(out=xs_sb[:], in_=x_scale.rearrange("(g p j) b -> p g (j b)", p=P, j=PACK))
-        load_e(2)
-        load_x(0, 0)
-        load_e(3)
-        load_e(4)
-        load_x(0, 1)
-        load_e(5)
-        load_e(6)
-        load_e(7)
+        load_x(0, 0, 1)
+        load_e(1, 1)
+        load_e(2, 2)
+        load_x(0, 1, 4)
+        load_e(4, 2)
+        load_w(0)
+        load_w(1)
+        load_e(6, 2)
+        load_w(2)
+        load_w(3)
+        load_x(1, 0, 4)
         nc.sync.dma_start(out=s_sb[:].bitcast(I32), in_=s_words.rearrange("g p n -> p g n").bitcast(I32))
         for q in range(4):
             nc.sync.dma_start(
@@ -107,41 +111,54 @@ def tile_proportionateleakyadjointloglmsupdate_d1p_kernel(
                 in_=s_scales[:, 4 * q : 4 * q + 4, :].rearrange("g r n -> r g n").bitcast(I32),
             )
         nc.sync.dma_start(out=g_sb[:], in_=g.rearrange("(g p j) -> p g j", p=P, j=PACK))
-        for ch in range(CHUNKS):
-            load_w(ch)
-        load_x(1, 0)
-        load_x(1, 1)
+        load_x(0, 4, 8)
+        load_x(1, 4, 8)
 
         c_bank = bank(6, [P, 4, P], F32, "c_bank")
         for i in range(4):
             nc.tensor.transpose(c_bank[:, i, :], c_words[:, i : i + 1].to_broadcast([P, P]), ident_f32[:])
-        c_all = keep.tile([P, 2, P, 2], F32, name="c_all")
-        nc.scalar.copy(out=c_all[:], in_=c_bank[:].rearrange("p (h u) r -> p u r h", u=2))
+        c_all = {count: keep.tile([P, 2, count, P, 2], F32, name="c_all%d" % count) for count in (1, 2)}
+        nc.scalar.copy(out=c_all[1][:, :, 0], in_=c_bank[:].rearrange("p (h u) r -> p u r h", u=2))
+
+        def double_c():
+            nc.scalar.copy(
+                out=c_all[2][:].rearrange("p u j r h -> p u j (r h)"),
+                in_=c_all[1][:].rearrange("p u j r h -> p u j (r h)").to_broadcast([P, 2, 2, 2 * P]),
+            )
 
         abs_e, signed_c, abs_bank, sc_bank, log_e, v_bf, v_codes, v_scales = {}, {}, {}, {}, {}, {}, {}, {}
 
-        def e_words(i):
-            return e_sb[i][:].bitcast(I32).rearrange("p (q u) -> p u q", u=2)
+        def e_words(i, count):
+            rows = e_sb[i // 2][:, i % 2 : i % 2 + count, :].rearrange("p j m -> p (j m)")
+            return rows.bitcast(I32).rearrange("p (q u) -> p u q", u=2)
 
-        def abs_of_e(i):
-            abs_e[i] = flow.tile([P, 2, M // 4], I32, name="abs_e")
-            nc.vector.tensor_scalar(out=abs_e[i][:], in0=e_words(i), scalar1=ABS_MASK, scalar2=None, op0=ALU.bitwise_and)
+        def abs_of_e(i, count):
+            words = flow.tile([P, 2, count, M // 4], I32, name="abs_e")
+            for j in range(count):
+                abs_e[i + j] = words[:, :, j, :]
+            nc.vector.tensor_scalar(
+                out=words[:].rearrange("p u j q -> p u (j q)"),
+                in0=e_words(i, count), scalar1=ABS_MASK, scalar2=None, op0=ALU.bitwise_and,
+            )
 
-        def sign_of_e(i):
-            signed_c[i] = flow.tile([P, 2, M // 4], I32, name="signed_c")
+        def sign_of_e(i, count):
+            words = flow.tile([P, 2, count, M // 4], I32, name="signed_c")
+            for j in range(count):
+                signed_c[i + j] = words[:, :, j, :]
             nc.vector.scalar_tensor_tensor(
-                out=signed_c[i][:],
-                in0=e_words(i),
+                out=words[:].rearrange("p u j q -> p u (j q)"),
+                in0=e_words(i, count),
                 scalar=SIGN_MASK,
-                in1=c_all[:].rearrange("p u r h -> p u (r h)").bitcast(I32),
+                in1=c_all[count][:].rearrange("p u j r h -> p u (j r h)").bitcast(I32),
                 op0=ALU.bitwise_and,
                 op1=ALU.bitwise_xor,
             )
 
         def turn(src, dst):
-            words = src[:].rearrange("p u q -> p (u q)").bitcast(F32)
-            for b in range(4):
-                nc.tensor.transpose(dst[:, b, :], words[:, b * P : (b + 1) * P], ident_f32[:])
+            for u in range(2):
+                for gm in range(M_PASSES):
+                    words = src[:, u, gm * P : (gm + 1) * P].bitcast(F32)
+                    nc.tensor.transpose(dst[:, 2 * u + gm, :], words, ident_f32[:])
 
         def turn_abs(i):
             abs_bank[i] = bank(i % 2, [P, 4, P], F32, "abs_bank")
@@ -155,36 +172,40 @@ def tile_proportionateleakyadjointloglmsupdate_d1p_kernel(
             return turned[:].rearrange("p b r -> p (b r)").bitcast(BF16).rearrange("p (u r e) -> p r u e", u=2, e=2)
 
         def log_of_abs(i):
-            log_e[i] = flow.tile([P, M], F32, name="log_e", bufs=2)
+            log_e[i] = flow.tile([P, M], F32, name="log_e", tag="log_e%d" % (i % 3), bufs=1)
             nc.scalar.activation(
                 out=log_e[i][:].rearrange("p (r u e) -> p r u e", u=2, e=2),
                 in_=as_values(abs_bank[i]), func=ACT.Ln, bias=1.0,
             )
 
         def make_v(i):
-            v_bf[i] = flow.tile([P, M], BF16, name="v_bf", align_bytes=64)
+            if i // 2 not in v_bf:
+                v_bf[i // 2] = flow.tile([P, 2, M], BF16, name="v_bf", align_bytes=64, bufs=2)
             nc.vector.tensor_tensor(
-                out=v_bf[i][:].rearrange("p (r u e) -> p r u e", u=2, e=2),
+                out=v_bf[i // 2][:, i % 2, :].rearrange("p (r u e) -> p r u e", u=2, e=2),
                 in0=log_e[i][:].rearrange("p (r u e) -> p r u e", u=2, e=2),
                 in1=as_values(sc_bank[i]), op=ALU.mult,
             )
 
-        def quantize_v(i):
-            v_codes[i] = keep.tile([P, M // PACK], U32, name="v_codes%d" % i, align_bytes=64)
-            v_scales[i] = keep.tile([P, M // PACK], U8, name="v_scales%d" % i, align_bytes=64)
-            nc.vector.quantize_mx(out=v_codes[i][:].bitcast(FP8X4), scales=v_scales[i][:], in_=v_bf[i][:])
+        def quantize_v(k):
+            v_codes[k] = keep.tile([P, 2 * M // PACK], U32, name="v_codes%d" % k, align_bytes=64)
+            v_scales[k] = keep.tile([P, 2 * M // PACK], U8, name="v_scales%d" % k, align_bytes=64)
+            nc.vector.quantize_mx(
+                out=v_codes[k][:].bitcast(FP8X4), scales=v_scales[k][:], in_=v_bf[k][:].rearrange("p j m -> p (j m)")
+            )
 
         f_bank, fg_bf, fg_codes, fg_scales = {}, {}, {}, {}
 
         def first_matmul(gt, lt):
-            f_bank[gt, lt] = bank(4 + lt % 2, [P, PACK, P], F32, "f_bank")
+            f_bank[gt, lt] = bank(lt if gt else 4 + lt % 2, [P, PACK, P], F32, "f_bank")
             for j in range(PACK):
-                i = gt * PACK + j
+                k = (gt * PACK + j) // 2
                 for gm in range(M_PASSES):
+                    cols = slice((j % 2 * M_PASSES + gm) * P, (j % 2 * M_PASSES + gm + 1) * P)
                     nc.tensor.matmul_mx(
                         out=f_bank[gt, lt][:, j, :],
-                        lhsT=v_codes[i][:, gm * P : (gm + 1) * P].bitcast(FP8X4),
-                        lhsT_scale=v_scales[i][:, gm * P : (gm + 1) * P],
+                        lhsT=v_codes[k][:, cols].bitcast(FP8X4),
+                        lhsT_scale=v_scales[k][:, cols],
                         rhs=s_sb[:, gm, 2 * lt * P : 2 * (lt + 1) * P].bitcast(FP4X4),
                         rhs_scale=s_scale_sb[:, gm, lt * P : (lt + 1) * P],
                         start=(gm == 0),
@@ -192,12 +213,12 @@ def tile_proportionateleakyadjointloglmsupdate_d1p_kernel(
                     )
 
         def make_fg(gt, lt):
-            if lt == 0:
+            if gt not in fg_bf:
                 fg_bf[gt] = keep.tile([P, L, PACK], BF16, name="fg_bf%d" % gt, align_bytes=64)
             nc.vector.tensor_tensor(
-                out=fg_bf[gt][:, lt * P : (lt + 1) * P, :].rearrange("p (c i) j -> p c j i", i=4),
-                in0=f_bank[gt, lt][:].rearrange("p j (c i) -> p c j i", i=4),
-                in1=g_sb[:, gt, :].unsqueeze(1).unsqueeze(3).to_broadcast([P, P // 4, PACK, 4]),
+                out=fg_bf[gt][:, lt * P : (lt + 1) * P, :].rearrange("p (c i) j -> p c j i", i=2),
+                in0=f_bank[gt, lt][:].rearrange("p j (c i) -> p c j i", i=2),
+                in1=g_sb[:, gt, :].unsqueeze(1).unsqueeze(3).to_broadcast([P, P // 2, PACK, 2]),
                 op=ALU.mult,
             )
 
@@ -212,25 +233,24 @@ def tile_proportionateleakyadjointloglmsupdate_d1p_kernel(
         x_wide, x_mixed, x_codes, x_scales = {}, {}, {}, {}
 
         def widen_x(st, gt):
-            x_wide[st, gt] = keep.tile([P, PACK, STRIP], BF16, name="x_wide%d%d" % (st, gt))
-            h, first = divmod(st * STRIP, HALF)
+            if st not in x_wide:
+                x_wide[st] = flow.tile([P, T_PASSES, PACK, STRIP], BF16, name="x_wide", tag="x_wide%d" % (st % 6), bufs=1)
             for j in range(PACK):
                 for b in range(STRIP // BLOCK):
                     col = j * (N // BLOCK) + st * (STRIP // BLOCK) + b
                     nc.scalar.activation(
-                        out=x_wide[st, gt][:, j, b * BLOCK : (b + 1) * BLOCK],
-                        in_=x_raw[h, gt][:, j, first + b * BLOCK : first + (b + 1) * BLOCK].bitcast(FP8),
+                        out=x_wide[st][:, gt, j, b * BLOCK : (b + 1) * BLOCK],
+                        in_=x_raw[st, gt][:, j, b * BLOCK : (b + 1) * BLOCK].bitcast(FP8),
                         func=ACT.Copy,
                         scale=xs_sb[:, gt, col : col + 1],
                     )
 
-        def mix_x(st, gt):
-            if gt == 0:
-                x_mixed[st] = flow.tile([P, T_PASSES, STRIP, PACK], BF16, name="x_mixed", align_bytes=64, bufs=3)
-            copy = nc.scalar.copy if (st, gt) in ON_SCALAR else nc.vector.tensor_copy
+        def mix_x(st):
+            x_mixed[st] = flow.tile([P, T_PASSES, STRIP, PACK], BF16, name="x_mixed", tag="x_mixed%d" % (st % 3), align_bytes=64, bufs=1)
+            copy = nc.scalar.copy if st in ON_SCALAR else nc.vector.tensor_copy
             copy(
-                out=x_mixed[st][:, gt].rearrange("p (c i) j -> p c j i", i=4),
-                in_=x_wide[st, gt][:].rearrange("p j (c i) -> p c j i", i=4),
+                out=x_mixed[st][:].rearrange("p g (c i) j -> p g c j i", i=4),
+                in_=x_wide[st][:].rearrange("p g j (c i) -> p g c j i", i=4),
             )
 
         def quantize_x(st):
@@ -244,28 +264,28 @@ def tile_proportionateleakyadjointloglmsupdate_d1p_kernel(
 
         abs_w = {}
 
-        def abs_of_w(ch):
-            abs_w[ch] = flow.tile([P, CHUNK // P, L], BF16, name="abs_w", bufs=2)
+        def abs_of_w(h):
+            if not abs_w:
+                abs_w[0] = keep.tile([P, N_TILES, L], BF16, name="abs_w", tag="gain1")
             nc.vector.tensor_scalar(
-                out=abs_w[ch][:].bitcast(I32), in0=w_sb[ch][:].bitcast(I32),
+                out=abs_w[0][:, 8 * h : 8 * h + 8, :].bitcast(I32), in0=w_sb[:, 8 * h : 8 * h + 8, :].bitcast(I32),
                 scalar1=ABS_MASK, scalar2=None, op0=ALU.bitwise_and,
             )
 
         gain_scale = keep.tile([P, L_TILES], F32, name="gain_scale")
-
         sums = {}
 
-        def column_sums(ch):
-            if ch == 0:
-                sums[0] = bank(6, [P, L_TILES, CHUNKS, 2], F32, "sums")
+        def column_sums(h):
+            if not sums:
+                sums[0] = bank(6, [P, L_TILES, 2, 2], F32, "sums")
             for lt in range(L_TILES):
-                for q in range(CHUNK // P):
+                for q in range(N_TILES // 2):
                     nc.tensor.matmul(
-                        out=sums[0][:, lt, ch, :],
-                        lhsT=abs_w[ch][:, q, lt * P : (lt + 1) * P],
+                        out=sums[0][:, lt, h, :],
+                        lhsT=abs_w[0][:, 8 * h + q, lt * P : (lt + 1) * P],
                         rhs=ones[:],
                         start=(q == 0),
-                        stop=(q == CHUNK // P - 1),
+                        stop=(q == N_TILES // 2 - 1),
                     )
 
         total = keep.tile([P, L_TILES], F32, name="total")
@@ -290,12 +310,12 @@ def tile_proportionateleakyadjointloglmsupdate_d1p_kernel(
             for i in range(HALF // P):
                 nc.tensor.transpose(
                     w_bank[h, lt][:, i * P : (i + 1) * P],
-                    w_sb[2 * h + i // 4][:, i % 4, lt * P : (lt + 1) * P],
+                    w_sb[:, 8 * h + i, lt * P : (lt + 1) * P],
                     ident_bf16[:],
                 )
 
         def make_gain(h, lt):
-            if lt == 0:
+            if h not in gain:
                 gain[h] = keep.tile([P, L_TILES, HALF], F32, name="gain%d" % h)
             nc.scalar.activation(out=gain[h][:, lt, :], in_=w_bank[h, lt][:], func=ACT.Abs, scale=gain_scale[:, lt : lt + 1])
 
@@ -315,7 +335,7 @@ def tile_proportionateleakyadjointloglmsupdate_d1p_kernel(
                     )
 
         def make_update(st, k):
-            update[st, k] = flow.tile([P, 2, STRIP], F32, name="update", bufs=6)
+            update[st, k] = flow.tile([P, 2, STRIP], F32, name="update", tag="update%d" % (st % 3 * 2 + k), bufs=1)
             h, first = divmod(st * STRIP, HALF)
             nc.vector.scalar_tensor_tensor(
                 out=update[st, k][:], in0=gain[h][:, 2 * k : 2 * k + 2, first : first + STRIP], scalar=GAIN,
@@ -324,57 +344,73 @@ def tile_proportionateleakyadjointloglmsupdate_d1p_kernel(
 
         def turn_back(st, q):
             i = 2 * st + q
-            out_bank[st, q] = bank(4 + (i % 4 if st >= WIDE_FROM else q), [P, L], F32, "out_bank")
-            nc.tensor.matmul(out=out_bank[st, q][:], lhsT=ident_bf16[:], rhs=w_sb[i // 4][:, i % 4, :], start=True, stop=False)
+            out_bank[st, q] = bank(4 + i % 4, [P, L], F32, "out_bank")
+            with_w = st not in FINISH_ON_VECTOR
+            if with_w:
+                nc.tensor.matmul(out=out_bank[st, q][:], lhsT=ident_bf16[:], rhs=w_sb[:, i, :], start=True, stop=False)
             for lt in range(L_TILES):
                 nc.tensor.matmul(
                     out=out_bank[st, q][:, lt * P : (lt + 1) * P],
                     lhsT=update[st, lt // 2][:, lt % 2, q * P : (q + 1) * P],
                     rhs=ident_f32[:],
                     is_transpose=True,
-                    start=False,
-                    stop=(lt == L_TILES - 1),
+                    start=not with_w,
+                    stop=(lt == L_TILES - 1 or not with_w),
                 )
+
+        leaked = {}
+
+        def leak_w(st):
+            leaked[st] = flow.tile([P, 2, L], F32, name="leaked", tag="log_e")
+            nc.scalar.activation(out=leaked[st][:], in_=w_sb[:, 2 * st : 2 * st + 2, :], func=ACT.Copy, scale=LEAK)
 
         def store(st, q):
             result = flow.tile([P, L], F32, name="result", bufs=6)
-            nc.scalar.activation(out=result[:], in_=out_bank[st, q][:], func=ACT.Copy, scale=LEAK)
+            if st in FINISH_ON_VECTOR:
+                nc.vector.scalar_tensor_tensor(
+                    out=result[:], in0=out_bank[st, q][:], scalar=LEAK, in1=leaked[st][:, q, :], op0=ALU.mult, op1=ALU.add
+                )
+            else:
+                nc.scalar.activation(out=result[:], in_=out_bank[st, q][:], func=ACT.Copy, scale=LEAK)
             row = st * STRIP + q * P
             nc.sync.dma_start(out=out[row : row + P, :], in_=result[:])
 
         pair, quad = range(2), range(4)
 
+        def rows_step(fn, i):
+            return (fn, i, 1) if i < 2 else (fn, i - i % 2, 2)
+
         def needs(step):
             fn, a = step[0], step[1:]
             if fn is turn_abs:
-                return [(abs_of_e,) + a, (log_of_abs, a[0] - 2)]
+                return [rows_step(abs_of_e, a[0]), (log_of_abs, a[0] - 2)]
             if fn is turn_sign:
-                return [(sign_of_e,) + a, (make_v, a[0] - 2)]
+                return [rows_step(sign_of_e, a[0]), (make_v, a[0] - 2)]
             if fn is abs_of_e:
-                return [(turn_abs, a[0] - 3)]
+                return [(turn_abs, a[0] - 4 + (a[0] > 4))]
             if fn is sign_of_e:
-                return [(turn_sign, a[0] - 3)]
+                return [(turn_sign, a[0] - 4 + (a[0] > 4))] + [(double_c,)] * (a[1] - 1)
             if fn is log_of_abs:
-                return [(turn_abs,) + a, (make_v, a[0] - 2)]
+                return [(turn_abs,) + a, (make_v, a[0] - 3)]
             if fn is make_v:
                 return [(log_of_abs,) + a, (turn_sign,) + a]
             if fn is first_matmul:
-                before = divmod(a[0] * L_TILES + a[1] - 2, L_TILES)
-                return [(quantize_v, a[0] * PACK + j) for j in quad] + [(make_fg,) + before]
+                free = [] if a[0] else [(make_fg, 0, a[1] - 2)]
+                return [(quantize_v, a[0] * 2 + k) for k in pair] + free
             if fn is make_fg:
                 return [(first_matmul,) + a]
             if fn is mix_x:
-                return [(widen_x,) + a, (mix_x, a[0], a[1] - 1), (quantize_x, a[0] - 3)]
+                return [(widen_x, a[0], gt) for gt in pair] + [(quantize_x, a[0] - 3)]
+            if fn is widen_x:
+                return [(mix_x, a[0] - 6)]
             if fn is quantize_x:
-                return [(mix_x, a[0], gt) for gt in pair]
-            if fn is abs_of_w:
-                return [(column_sums, a[0] - 2)]
+                return [(mix_x,) + a]
             if fn is column_sums:
                 return [(abs_of_w,) + a]
             if fn is add_sums:
-                return [(column_sums, ch) for ch in quad]
+                return [(column_sums, h) for h in pair]
             if fn is turn_w:
-                return [(add_sums,), (make_gain,) + divmod(a[0] * L_TILES + a[1] - 2, L_TILES)]
+                return [(add_sums,)] * (1 - a[1] % 2) + [(make_gain,) + divmod(a[0] * L_TILES + a[1] - 2, L_TILES)]
             if fn is make_gain:
                 return [(turn_w,) + a, (invert_denom,)]
             if fn is second_matmul:
@@ -385,47 +421,17 @@ def tile_proportionateleakyadjointloglmsupdate_d1p_kernel(
             if fn is turn_back:
                 free = [(make_gain, 1, 2 + a[1])] if a[0] == WIDE_FROM else [(store, a[0] - (2 if a[0] > WIDE_FROM else 1), a[1])]
                 return [(make_update, a[0], k) for k in pair] + free
+            if fn is leak_w:
+                return [(make_v, TOKEN_TILES - 1)]
             if fn is store:
-                return [(turn_back,) + a]
+                return [(turn_back,) + a] + [(leak_w, st) for st in FINISH_ON_VECTOR if st == a[0]]
             return []
 
-        vector = [(abs_of_e, 0), (abs_of_e, 1), (sign_of_e, 0)]
-        for i in range(TOKEN_TILES):
-            vector += [(abs_of_e, i + 2), (sign_of_e, i + 1), (abs_of_w, i - WL), (make_v, i), (quantize_v, i - 1)]
-            vector += [(make_fg, 0, i - 5)]
-        vector += [(add_sums,), (quantize_v, 7), (make_denom,), (make_fg, 0, 3), (invert_denom,)]
-        vector += [(mix_x, 0, 0), (quantize_fg, 0), (mix_x, 0, 1), (make_fg, 1, 0), (make_fg, 1, 1), (quantize_x, 0)]
-        vector += [(mix_x, 1, 0), (make_fg, 1, 2), (make_fg, 1, 3), (mix_x, 1, 1), (quantize_fg, 1), (quantize_x, 1)]
-        vector += [(mix_x, 2, 0), (mix_x, 2, 1), (make_update, 0, 0), (quantize_x, 2), (make_update, 0, 1)]
-        vector += [(make_update, 1, 0), (make_update, 1, 1)]
-        for st in range(2, STRIPS):
-            vector += [(mix_x, st + 1, 0), (mix_x, st + 1, 1), (make_update, st, 0), (quantize_x, st + 1), (make_update, st, 1)]
+        vector = [(abs_of_e, 0, 1), (sign_of_e, 0, 1), (sign_of_e, 1, 1), (abs_of_e, 1, 1), (sign_of_e, 2, 2), (abs_of_e, 2, 2), (make_v, 0), (sign_of_e, 4, 2), (make_v, 1), (abs_of_e, 4, 2), (quantize_v, 0), (make_v, 2), (make_v, 3), (abs_of_e, 6, 2), (quantize_v, 1), (abs_of_w, 0), (sign_of_e, 6, 2), (abs_of_w, 1), (make_v, 4), (make_fg, 0, 0), (make_v, 5), (mix_x, 0), (add_sums,), (make_fg, 0, 1), (make_denom,), (quantize_v, 2), (invert_denom,), (make_v, 7), (make_v, 6), (make_fg, 0, 2), (quantize_v, 3), (make_fg, 0, 3), (mix_x, 1), (make_fg, 1, 1), (make_fg, 1, 0), (quantize_x, 0), (make_fg, 1, 3), (make_fg, 1, 2), (quantize_fg, 0), (quantize_fg, 1), (quantize_x, 1), (mix_x, 3), (mix_x, 2), (make_update, 0, 1), (quantize_x, 2), (make_update, 0, 0), (quantize_x, 3), (make_update, 1, 0), (make_update, 2, 0), (make_update, 1, 1), (make_update, 2, 1), (mix_x, 4), (mix_x, 5), (quantize_x, 4), (quantize_x, 5), (make_update, 3, 0), (make_update, 3, 1), (make_update, 4, 1), (make_update, 5, 0), (make_update, 5, 1), (make_update, 4, 0), (mix_x, 6), (quantize_x, 7), (quantize_x, 6), (make_update, 7, 0), (make_update, 6, 0), (make_update, 6, 1), (make_update, 7, 1)]
+        scalar = [(double_c,), (log_of_abs, 0), (widen_x, 3, 0), (log_of_abs, 1), (widen_x, 2, 0), (log_of_abs, 2), (log_of_abs, 3), (widen_x, 0, 0), (log_of_abs, 5), (log_of_abs, 4), (widen_x, 3, 1), (log_of_abs, 6), (widen_x, 0, 1), (widen_x, 1, 0), (log_of_abs, 7), (widen_x, 4, 1), (widen_x, 2, 1), (make_gain, 0, 0), (widen_x, 1, 1), (widen_x, 5, 0), (make_gain, 0, 1), (widen_x, 4, 0), (make_gain, 0, 3), (make_gain, 0, 2), (widen_x, 7, 1), (make_gain, 1, 1), (make_gain, 1, 0), (widen_x, 5, 1), (widen_x, 6, 1), (make_gain, 1, 3), (make_gain, 1, 2), (store, 0, 1), (store, 0, 0), (widen_x, 6, 0), (store, 2, 1), (widen_x, 7, 0), (store, 2, 0), (store, 1, 0), (store, 1, 1), (mix_x, 7), (store, 3, 1), (store, 3, 0), (store, 4, 1), (store, 5, 0), (store, 5, 1), (store, 4, 0), (store, 6, 0), (store, 6, 1), (store, 7, 0), (store, 7, 1)]
+        tensor = [(turn_abs, 0), (turn_sign, 0), (turn_abs, 1), (turn_sign, 1), (turn_sign, 2), (turn_abs, 2), (turn_abs, 3), (turn_sign, 3), (turn_w, 0, 1), (turn_abs, 5), (turn_abs, 4), (turn_sign, 4), (turn_abs, 6), (turn_sign, 5), (first_matmul, 0, 0), (turn_abs, 7), (first_matmul, 0, 1), (column_sums, 1), (column_sums, 0), (turn_sign, 6), (turn_sign, 7), (turn_w, 0, 0), (first_matmul, 0, 3), (first_matmul, 0, 2), (turn_w, 0, 2), (first_matmul, 1, 0), (first_matmul, 1, 1), (first_matmul, 1, 2), (turn_w, 0, 3), (first_matmul, 1, 3), (turn_w, 1, 1), (turn_w, 1, 0), (second_matmul, 0, 0), (second_matmul, 1, 0), (second_matmul, 0, 1), (turn_w, 1, 3), (turn_w, 1, 2), (second_matmul, 1, 1), (second_matmul, 2, 1), (second_matmul, 2, 0), (turn_back, 0, 0), (turn_back, 0, 1), (second_matmul, 3, 0), (turn_back, 1, 1), (turn_back, 2, 1), (turn_back, 1, 0), (turn_back, 2, 0), (second_matmul, 3, 1), (second_matmul, 4, 0), (second_matmul, 4, 1), (second_matmul, 5, 0), (second_matmul, 5, 1), (turn_back, 3, 1), (turn_back, 3, 0), (turn_back, 4, 1), (turn_back, 4, 0), (turn_back, 5, 1), (turn_back, 5, 0), (second_matmul, 7, 0), (second_matmul, 6, 0), (second_matmul, 6, 1), (second_matmul, 7, 1), (turn_back, 6, 0), (turn_back, 6, 1), (turn_back, 7, 0), (turn_back, 7, 1)]
 
-        vector = [step for step in vector if step[0] is not mix_x or step[1:] not in ON_SCALAR]
-
-        wides = [(widen_x, st, gt) for st in range(STRIPS) for gt in pair]
-        gains = [(make_gain, h, lt) for h in pair for lt in quad]
-        scalar = [(log_of_abs, 0)]
-        for i in range(TOKEN_TILES):
-            scalar += [(log_of_abs, i + 1), wides[i]]
-        scalar += wides[8:11] + gains[0:2] + wides[11:12] + gains[2:4] + wides[12:14]
-        extra = [gains[4:6], wides[14:16], gains[6:8], [(mix_x, 7, 0)], [(mix_x, 7, 1)], [], [], []]
-        for st in range(STRIPS):
-            scalar += extra[st] + [(store, st, q) for q in pair]
-
-        turns = [(turn_w, h, lt) for h in pair for lt in quad]
-        tensor = [(turn_abs, 0), (turn_abs, 1), (turn_sign, 0)]
-        for i in range(TOKEN_TILES):
-            tensor += [(turn_abs, i + 2), (turn_sign, i + 1), (column_sums, i - WL), (first_matmul, 0, i - 4)]
-        tensor += turns[0:2] + [(first_matmul, 1, 0), (first_matmul, 1, 1)] + turns[2:3]
-        tensor += [(first_matmul, 1, 2), (first_matmul, 1, 3)] + turns[3:5]
-        tensor += [(second_matmul, st, k) for st in pair for k in pair] + turns[5:6]
-        tensor += [(turn_back, 0, q) for q in pair]
-        for st in range(2, STRIPS + 1):
-            tensor += [(second_matmul, st, k) for k in pair] + [(turn_back, st - 1, q) for q in pair]
-            tensor += turns[6:8] if st == 2 else []
-
-        counts = {abs_of_w: CHUNKS, column_sums: CHUNKS}
+        counts = {}
 
         def real(step):
             return all(0 <= k < counts.get(step[0], STRIPS) for k in step[1:])

from contextlib import ExitStack

import concourse.mybir as mybir
from concourse.masks import make_identity

T, M, N, L = 1024, 1024, 2048, 512
FLOPS = 2 * T * M * L + 2 * T * N * L

F32 = mybir.dt.float32
BF16 = mybir.dt.bfloat16
I32 = mybir.dt.int32
U32 = mybir.dt.uint32
U8 = mybir.dt.uint8
FP8 = mybir.dt.float8_e4m3fn
FP8X4 = mybir.dt.float8_e4m3fn_x4
FP4X4 = mybir.dt.float4_e2m1fn_x4
ALU = mybir.AluOpType
ACT = mybir.ActivationFunctionType

P = 128
PACK = 4
K_PASS = P * PACK
T_PASSES = T // K_PASS
M_PASSES = M // K_PASS
TOKEN_TILES = T // P
L_TILES = L // P
N_TILES = N // P
CHUNK = 512
CHUNKS = N // CHUNK
BLOCK = 128
HALF = N // 2
STRIP = 256
WL = 4
WIDE_FROM = 1
ON_SCALAR = [7]
FINISH_ON_VECTOR = []
STRIPS = N // STRIP

ABS_MASK = 0x7FFF7FFF
SIGN_MASK = 0x80008000 - (1 << 32)
LEAK = 0.9
GAIN = 0.25 / 32.0 / LEAK


def tile_proportionateleakyadjointloglmsupdate_d1p_kernel(
    tc, x_bytes, x_scale, e, c, s_words, s_scales, g, w, out
):
    nc = tc.nc
    with ExitStack() as ctx:
        keep = ctx.enter_context(tc.tile_pool(name="keep", bufs=1))
        flow = ctx.enter_context(tc.tile_pool(name="flow", bufs=3))
        psum = ctx.enter_context(tc.psum_pool(name="psum", bufs=1))
        ctx.enter_context(tc.manual_schedule())

        def bank(index, shape, dtype, name):
            return psum.tile(shape, dtype, name=name, tag="bank%d" % index)

        ident_f32 = keep.tile([P, P], F32, name="ident_f32")
        ident_bf16 = keep.tile([P, P], BF16, name="ident_bf16")
        make_identity(nc, ident_f32[:])
        make_identity(nc, ident_bf16[:])
        ones = keep.tile([P, 2], BF16, name="ones")
        nc.vector.memset(ones[:], 1.0)
        s_scale_sb = keep.tile([P, M_PASSES, L], U8, name="s_scale_sb", align_bytes=64)
        nc.vector.memset(s_scale_sb[:].rearrange("p g n -> p (g n)").bitcast(I32), 0)
        warm = keep.tile([P, 1], F32, name="warm")
        nc.scalar.activation(out=warm[:], in_=ones[:, 0:1], func=ACT.Ln)

        c_words = keep.tile([P, 4], F32, name="c_words")
        nc.sync.dma_start(out=c_words[:].bitcast(BF16), in_=c.rearrange("(p i) -> p i", p=P))
        e_rows = e.rearrange("(g p j) m -> g p j m", p=P, j=PACK)
        e_sb = [keep.tile([P, 2, M], BF16, name="e_sb%d" % i) for i in range(TOKEN_TILES // 2)]
        x_rows = x_bytes.rearrange("(g p j) n -> g p j n", p=P, j=PACK)
        x_raw = {}
        xs_sb = keep.tile([P, T_PASSES, PACK * 16], F32, name="xs_sb")
        s_sb = keep.tile([P, M_PASSES, 2 * L], U8, name="s_sb", align_bytes=64)
        g_sb = keep.tile([P, T_PASSES, PACK], BF16, name="g_sb")
        w_rows = w.rearrange("(c q p) l -> c p q l", p=P, q=CHUNK // P)
        w_sb = keep.tile([P, N_TILES, L], BF16, name="w_sb")

        def load_e(i, count):
            gt, j = divmod(i, PACK)
            nc.sync.dma_start(out=e_sb[i // 2][:, i % 2 : i % 2 + count, :], in_=e_rows[gt][:, j : j + count, :])

        def load_x(gt, first, last):
            raw = keep.tile([P, PACK, (last - first) * STRIP], U8, name="x_raw%d%d" % (gt, first))
            nc.sync.dma_start(out=raw[:], in_=x_rows[gt][:, :, first * STRIP : last * STRIP])
            for st in range(first, last):
                x_raw[st, gt] = raw[:, :, (st - first) * STRIP : (st - first + 1) * STRIP]

        def load_w(ch):
            nc.sync.dma_start(out=w_sb[:, 4 * ch : 4 * ch + 4, :], in_=w_rows[ch])

        load_e(0, 1)
        nc.sync.dma_start(out=xs_sb[:], in_=x_scale.rearrange("(g p j) b -> p g (j b)", p=P, j=PACK))
        load_x(0, 0, 1)
        load_e(1, 1)
        load_e(2, 2)
        load_x(0, 1, 4)
        load_e(4, 2)
        load_w(0)
        load_w(1)
        load_e(6, 2)
        load_w(2)
        load_w(3)
        load_x(1, 0, 4)
        nc.sync.dma_start(out=s_sb[:].bitcast(I32), in_=s_words.rearrange("g p n -> p g n").bitcast(I32))
        for q in range(4):
            nc.sync.dma_start(
                out=s_scale_sb[32 * q : 32 * q + 4, :, :].bitcast(I32),
                in_=s_scales[:, 4 * q : 4 * q + 4, :].rearrange("g r n -> r g n").bitcast(I32),
            )
        nc.sync.dma_start(out=g_sb[:], in_=g.rearrange("(g p j) -> p g j", p=P, j=PACK))
        load_x(0, 4, 8)
        load_x(1, 4, 8)

        c_bank = bank(6, [P, 4, P], F32, "c_bank")
        for i in range(4):
            nc.tensor.transpose(c_bank[:, i, :], c_words[:, i : i + 1].to_broadcast([P, P]), ident_f32[:])
        c_all = {count: keep.tile([P, 2, count, P, 2], F32, name="c_all%d" % count) for count in (1, 2)}
        nc.scalar.copy(out=c_all[1][:, :, 0], in_=c_bank[:].rearrange("p (h u) r -> p u r h", u=2))

        def double_c():
            nc.scalar.copy(
                out=c_all[2][:].rearrange("p u j r h -> p u j (r h)"),
                in_=c_all[1][:].rearrange("p u j r h -> p u j (r h)").to_broadcast([P, 2, 2, 2 * P]),
            )

        abs_e, signed_c, abs_bank, sc_bank, log_e, v_bf, v_codes, v_scales = {}, {}, {}, {}, {}, {}, {}, {}

        def e_words(i, count):
            rows = e_sb[i // 2][:, i % 2 : i % 2 + count, :].rearrange("p j m -> p (j m)")
            return rows.bitcast(I32).rearrange("p (q u) -> p u q", u=2)

        def abs_of_e(i, count):
            words = flow.tile([P, 2, count, M // 4], I32, name="abs_e")
            for j in range(count):
                abs_e[i + j] = words[:, :, j, :]
            nc.vector.tensor_scalar(
                out=words[:].rearrange("p u j q -> p u (j q)"),
                in0=e_words(i, count), scalar1=ABS_MASK, scalar2=None, op0=ALU.bitwise_and,
            )

        def sign_of_e(i, count):
            words = flow.tile([P, 2, count, M // 4], I32, name="signed_c")
            for j in range(count):
                signed_c[i + j] = words[:, :, j, :]
            nc.vector.scalar_tensor_tensor(
                out=words[:].rearrange("p u j q -> p u (j q)"),
                in0=e_words(i, count),
                scalar=SIGN_MASK,
                in1=c_all[count][:].rearrange("p u j r h -> p u (j r h)").bitcast(I32),
                op0=ALU.bitwise_and,
                op1=ALU.bitwise_xor,
            )

        def turn(src, dst):
            for u in range(2):
                for gm in range(M_PASSES):
                    words = src[:, u, gm * P : (gm + 1) * P].bitcast(F32)
                    nc.tensor.transpose(dst[:, 2 * u + gm, :], words, ident_f32[:])

        def turn_abs(i):
            abs_bank[i] = bank(i % 2, [P, 4, P], F32, "abs_bank")
            turn(abs_e[i], abs_bank[i])

        def turn_sign(i):
            sc_bank[i] = bank(2 + i % 2, [P, 4, P], F32, "sc_bank")
            turn(signed_c[i], sc_bank[i])

        def as_values(turned):
            return turned[:].rearrange("p b r -> p (b r)").bitcast(BF16).rearrange("p (u r e) -> p r u e", u=2, e=2)

        def log_of_abs(i):
            log_e[i] = flow.tile([P, M], F32, name="log_e", tag="log_e%d" % (i % 3), bufs=1)
            nc.scalar.activation(
                out=log_e[i][:].rearrange("p (r u e) -> p r u e", u=2, e=2),
                in_=as_values(abs_bank[i]), func=ACT.Ln, bias=1.0,
            )

        def make_v(i):
            if i // 2 not in v_bf:
                v_bf[i // 2] = flow.tile([P, 2, M], BF16, name="v_bf", align_bytes=64, bufs=2)
            nc.vector.tensor_tensor(
                out=v_bf[i // 2][:, i % 2, :].rearrange("p (r u e) -> p r u e", u=2, e=2),
                in0=log_e[i][:].rearrange("p (r u e) -> p r u e", u=2, e=2),
                in1=as_values(sc_bank[i]), op=ALU.mult,
            )

        def quantize_v(k):
            v_codes[k] = keep.tile([P, 2 * M // PACK], U32, name="v_codes%d" % k, align_bytes=64)
            v_scales[k] = keep.tile([P, 2 * M // PACK], U8, name="v_scales%d" % k, align_bytes=64)
            nc.vector.quantize_mx(
                out=v_codes[k][:].bitcast(FP8X4), scales=v_scales[k][:], in_=v_bf[k][:].rearrange("p j m -> p (j m)")
            )

        f_bank, fg_bf, fg_codes, fg_scales = {}, {}, {}, {}

        def first_matmul(gt, lt):
            f_bank[gt, lt] = bank(lt if gt else 4 + lt % 2, [P, PACK, P], F32, "f_bank")
            for j in range(PACK):
                k = (gt * PACK + j) // 2
                for gm in range(M_PASSES):
                    cols = slice((j % 2 * M_PASSES + gm) * P, (j % 2 * M_PASSES + gm + 1) * P)
                    nc.tensor.matmul_mx(
                        out=f_bank[gt, lt][:, j, :],
                        lhsT=v_codes[k][:, cols].bitcast(FP8X4),
                        lhsT_scale=v_scales[k][:, cols],
                        rhs=s_sb[:, gm, 2 * lt * P : 2 * (lt + 1) * P].bitcast(FP4X4),
                        rhs_scale=s_scale_sb[:, gm, lt * P : (lt + 1) * P],
                        start=(gm == 0),
                        stop=(gm == M_PASSES - 1),
                    )

        def make_fg(gt, lt):
            if gt not in fg_bf:
                fg_bf[gt] = keep.tile([P, L, PACK], BF16, name="fg_bf%d" % gt, align_bytes=64)
            nc.vector.tensor_tensor(
                out=fg_bf[gt][:, lt * P : (lt + 1) * P, :].rearrange("p (c i) j -> p c j i", i=2),
                in0=f_bank[gt, lt][:].rearrange("p j (c i) -> p c j i", i=2),
                in1=g_sb[:, gt, :].unsqueeze(1).unsqueeze(3).to_broadcast([P, P // 2, PACK, 2]),
                op=ALU.mult,
            )

        def quantize_fg(gt):
            fg_codes[gt] = keep.tile([P, L], U32, name="fg_codes%d" % gt, align_bytes=64)
            fg_scales[gt] = keep.tile([P, L], U8, name="fg_scales%d" % gt, align_bytes=64)
            nc.vector.quantize_mx(
                out=fg_codes[gt][:].bitcast(FP8X4), scales=fg_scales[gt][:],
                in_=fg_bf[gt][:].rearrange("p l j -> p (l j)"),
            )

        x_wide, x_mixed, x_codes, x_scales = {}, {}, {}, {}

        def widen_x(st, gt):
            if st not in x_wide:
                x_wide[st] = flow.tile([P, T_PASSES, PACK, STRIP], BF16, name="x_wide", tag="x_wide%d" % (st % 6), bufs=1)
            for j in range(PACK):
                for b in range(STRIP // BLOCK):
                    col = j * (N // BLOCK) + st * (STRIP // BLOCK) + b
                    nc.scalar.activation(
                        out=x_wide[st][:, gt, j, b * BLOCK : (b + 1) * BLOCK],
                        in_=x_raw[st, gt][:, j, b * BLOCK : (b + 1) * BLOCK].bitcast(FP8),
                        func=ACT.Copy,
                        scale=xs_sb[:, gt, col : col + 1],
                    )

        def mix_x(st):
            x_mixed[st] = flow.tile([P, T_PASSES, STRIP, PACK], BF16, name="x_mixed", tag="x_mixed%d" % (st % 3), align_bytes=64, bufs=1)
            copy = nc.scalar.copy if st in ON_SCALAR else nc.vector.tensor_copy
            copy(
                out=x_mixed[st][:].rearrange("p g (c i) j -> p g c j i", i=4),
                in_=x_wide[st][:].rearrange("p g j (c i) -> p g c j i", i=4),
            )

        def quantize_x(st):
            x_codes[st] = keep.tile([P, T_PASSES, STRIP], U32, name="x_codes%d" % st, align_bytes=64)
            x_scales[st] = keep.tile([P, T_PASSES, STRIP], U8, name="x_scales%d" % st, align_bytes=64)
            nc.vector.quantize_mx(
                out=x_codes[st][:].rearrange("p g n -> p (g n)").bitcast(FP8X4),
                scales=x_scales[st][:].rearrange("p g n -> p (g n)"),
                in_=x_mixed[st][:].rearrange("p g n j -> p (g n j)"),
            )

        abs_w = {}

        def abs_of_w(h):
            if not abs_w:
                abs_w[0] = keep.tile([P, N_TILES, L], BF16, name="abs_w", tag="gain1")
            nc.vector.tensor_scalar(
                out=abs_w[0][:, 8 * h : 8 * h + 8, :].bitcast(I32), in0=w_sb[:, 8 * h : 8 * h + 8, :].bitcast(I32),
                scalar1=ABS_MASK, scalar2=None, op0=ALU.bitwise_and,
            )

        gain_scale = keep.tile([P, L_TILES], F32, name="gain_scale")
        sums = {}

        def column_sums(h):
            if not sums:
                sums[0] = bank(6, [P, L_TILES, 2, 2], F32, "sums")
            for lt in range(L_TILES):
                for q in range(N_TILES // 2):
                    nc.tensor.matmul(
                        out=sums[0][:, lt, h, :],
                        lhsT=abs_w[0][:, 8 * h + q, lt * P : (lt + 1) * P],
                        rhs=ones[:],
                        start=(q == 0),
                        stop=(q == N_TILES // 2 - 1),
                    )

        total = keep.tile([P, L_TILES], F32, name="total")
        denom = keep.tile([P, L_TILES], F32, name="denom")

        def add_sums():
            nc.vector.tensor_reduce(out=total[:], in_=sums[0][:, :, :, 0], axis=mybir.AxisListType.X, op=ALU.add)

        def make_denom():
            nc.vector.tensor_scalar(
                out=denom[:], in0=total[:], scalar1=1.0 / (N * GAIN), scalar2=0.001 / GAIN,
                op0=ALU.mult, op1=ALU.add,
            )

        def invert_denom():
            nc.vector.reciprocal(out=gain_scale[:], in_=denom[:])

        w_bank, gain, acc, update, out_bank = {}, {}, {}, {}, {}

        def turn_w(h, lt):
            w_bank[h, lt] = bank(6 + lt % 2, [P, HALF], BF16, "w_bank")
            for i in range(HALF // P):
                nc.tensor.transpose(
                    w_bank[h, lt][:, i * P : (i + 1) * P],
                    w_sb[:, 8 * h + i, lt * P : (lt + 1) * P],
                    ident_bf16[:],
                )

        def make_gain(h, lt):
            if h not in gain:
                gain[h] = keep.tile([P, L_TILES, HALF], F32, name="gain%d" % h)
            nc.scalar.activation(out=gain[h][:, lt, :], in_=w_bank[h, lt][:], func=ACT.Abs, scale=gain_scale[:, lt : lt + 1])

        def second_matmul(st, k):
            acc[st, k] = bank(st % 2 * 2 + k, [P, 2, STRIP], F32, "acc")
            for side in range(2):
                lt = 2 * k + side
                for gt in range(T_PASSES):
                    nc.tensor.matmul_mx(
                        out=acc[st, k][:, side, :],
                        lhsT=fg_codes[gt][:, lt * P : (lt + 1) * P].bitcast(FP8X4),
                        lhsT_scale=fg_scales[gt][:, lt * P : (lt + 1) * P],
                        rhs=x_codes[st][:, gt, :].bitcast(FP8X4),
                        rhs_scale=x_scales[st][:, gt, :],
                        start=(gt == 0),
                        stop=(gt == T_PASSES - 1),
                    )

        def make_update(st, k):
            update[st, k] = flow.tile([P, 2, STRIP], F32, name="update", tag="update%d" % (st % 3 * 2 + k), bufs=1)
            h, first = divmod(st * STRIP, HALF)
            nc.vector.scalar_tensor_tensor(
                out=update[st, k][:], in0=gain[h][:, 2 * k : 2 * k + 2, first : first + STRIP], scalar=GAIN,
                in1=acc[st, k][:], op0=ALU.add, op1=ALU.mult,
            )

        def turn_back(st, q):
            i = 2 * st + q
            out_bank[st, q] = bank(4 + i % 4, [P, L], F32, "out_bank")
            with_w = st not in FINISH_ON_VECTOR
            if with_w:
                nc.tensor.matmul(out=out_bank[st, q][:], lhsT=ident_bf16[:], rhs=w_sb[:, i, :], start=True, stop=False)
            for lt in range(L_TILES):
                nc.tensor.matmul(
                    out=out_bank[st, q][:, lt * P : (lt + 1) * P],
                    lhsT=update[st, lt // 2][:, lt % 2, q * P : (q + 1) * P],
                    rhs=ident_f32[:],
                    is_transpose=True,
                    start=not with_w,
                    stop=(lt == L_TILES - 1 or not with_w),
                )

        leaked = {}

        def leak_w(st):
            leaked[st] = flow.tile([P, 2, L], F32, name="leaked", tag="log_e")
            nc.scalar.activation(out=leaked[st][:], in_=w_sb[:, 2 * st : 2 * st + 2, :], func=ACT.Copy, scale=LEAK)

        def store(st, q):
            result = flow.tile([P, L], F32, name="result", bufs=6)
            if st in FINISH_ON_VECTOR:
                nc.vector.scalar_tensor_tensor(
                    out=result[:], in0=out_bank[st, q][:], scalar=LEAK, in1=leaked[st][:, q, :], op0=ALU.mult, op1=ALU.add
                )
            else:
                nc.scalar.activation(out=result[:], in_=out_bank[st, q][:], func=ACT.Copy, scale=LEAK)
            row = st * STRIP + q * P
            nc.sync.dma_start(out=out[row : row + P, :], in_=result[:])

        pair, quad = range(2), range(4)

        def rows_step(fn, i):
            return (fn, i, 1) if i < 2 else (fn, i - i % 2, 2)

        def needs(step):
            fn, a = step[0], step[1:]
            if fn is turn_abs:
                return [rows_step(abs_of_e, a[0]), (log_of_abs, a[0] - 2)]
            if fn is turn_sign:
                return [rows_step(sign_of_e, a[0]), (make_v, a[0] - 2)]
            if fn is abs_of_e:
                return [(turn_abs, a[0] - 4 + (a[0] > 4))]
            if fn is sign_of_e:
                return [(turn_sign, a[0] - 4 + (a[0] > 4))] + [(double_c,)] * (a[1] - 1)
            if fn is log_of_abs:
                return [(turn_abs,) + a, (make_v, a[0] - 3)]
            if fn is make_v:
                return [(log_of_abs,) + a, (turn_sign,) + a]
            if fn is first_matmul:
                free = [] if a[0] else [(make_fg, 0, a[1] - 2)]
                return [(quantize_v, a[0] * 2 + k) for k in pair] + free
            if fn is make_fg:
                return [(first_matmul,) + a]
            if fn is mix_x:
                return [(widen_x, a[0], gt) for gt in pair] + [(quantize_x, a[0] - 3)]
            if fn is widen_x:
                return [(mix_x, a[0] - 6)]
            if fn is quantize_x:
                return [(mix_x,) + a]
            if fn is column_sums:
                return [(abs_of_w,) + a]
            if fn is add_sums:
                return [(column_sums, h) for h in pair]
            if fn is turn_w:
                return [(add_sums,)] * (1 - a[1] % 2) + [(make_gain,) + divmod(a[0] * L_TILES + a[1] - 2, L_TILES)]
            if fn is make_gain:
                return [(turn_w,) + a, (invert_denom,)]
            if fn is second_matmul:
                return [(quantize_x, a[0]), (quantize_fg, 0), (quantize_fg, 1), (make_update, a[0] - 2, a[1])]
            if fn is make_update:
                gains = [(make_gain, a[0] * STRIP // HALF, 2 * a[1] + side) for side in pair]
                return [(second_matmul,) + a] + gains + [(turn_back, a[0] - 3, q) for q in pair]
            if fn is turn_back:
                free = [(make_gain, 1, 2 + a[1])] if a[0] == WIDE_FROM else [(store, a[0] - (2 if a[0] > WIDE_FROM else 1), a[1])]
                return [(make_update, a[0], k) for k in pair] + free
            if fn is leak_w:
                return [(make_v, TOKEN_TILES - 1)]
            if fn is store:
                return [(turn_back,) + a] + [(leak_w, st) for st in FINISH_ON_VECTOR if st == a[0]]
            return []

        vector = [(abs_of_e, 0, 1), (sign_of_e, 0, 1), (sign_of_e, 1, 1), (abs_of_e, 1, 1), (sign_of_e, 2, 2), (abs_of_e, 2, 2), (make_v, 0), (sign_of_e, 4, 2), (make_v, 1), (abs_of_e, 4, 2), (quantize_v, 0), (make_v, 2), (make_v, 3), (abs_of_e, 6, 2), (quantize_v, 1), (abs_of_w, 0), (sign_of_e, 6, 2), (abs_of_w, 1), (make_v, 4), (make_fg, 0, 0), (make_v, 5), (mix_x, 0), (add_sums,), (make_fg, 0, 1), (make_denom,), (quantize_v, 2), (invert_denom,), (make_v, 7), (make_v, 6), (make_fg, 0, 2), (quantize_v, 3), (make_fg, 0, 3), (mix_x, 1), (make_fg, 1, 1), (make_fg, 1, 0), (quantize_x, 0), (make_fg, 1, 3), (make_fg, 1, 2), (quantize_fg, 0), (quantize_fg, 1), (quantize_x, 1), (mix_x, 3), (mix_x, 2), (make_update, 0, 1), (quantize_x, 2), (make_update, 0, 0), (quantize_x, 3), (make_update, 1, 0), (make_update, 2, 0), (make_update, 1, 1), (make_update, 2, 1), (mix_x, 4), (mix_x, 5), (quantize_x, 4), (quantize_x, 5), (make_update, 3, 0), (make_update, 3, 1), (make_update, 4, 1), (make_update, 5, 0), (make_update, 5, 1), (make_update, 4, 0), (mix_x, 6), (quantize_x, 7), (quantize_x, 6), (make_update, 7, 0), (make_update, 6, 0), (make_update, 6, 1), (make_update, 7, 1)]
        scalar = [(double_c,), (log_of_abs, 0), (widen_x, 3, 0), (log_of_abs, 1), (widen_x, 2, 0), (log_of_abs, 2), (log_of_abs, 3), (widen_x, 0, 0), (log_of_abs, 5), (log_of_abs, 4), (widen_x, 3, 1), (log_of_abs, 6), (widen_x, 0, 1), (widen_x, 1, 0), (log_of_abs, 7), (widen_x, 4, 1), (widen_x, 2, 1), (make_gain, 0, 0), (widen_x, 1, 1), (widen_x, 5, 0), (make_gain, 0, 1), (widen_x, 4, 0), (make_gain, 0, 3), (make_gain, 0, 2), (widen_x, 7, 1), (make_gain, 1, 1), (make_gain, 1, 0), (widen_x, 5, 1), (widen_x, 6, 1), (make_gain, 1, 3), (make_gain, 1, 2), (store, 0, 1), (store, 0, 0), (widen_x, 6, 0), (store, 2, 1), (widen_x, 7, 0), (store, 2, 0), (store, 1, 0), (store, 1, 1), (mix_x, 7), (store, 3, 1), (store, 3, 0), (store, 4, 1), (store, 5, 0), (store, 5, 1), (store, 4, 0), (store, 6, 0), (store, 6, 1), (store, 7, 0), (store, 7, 1)]
        tensor = [(turn_abs, 0), (turn_sign, 0), (turn_abs, 1), (turn_sign, 1), (turn_sign, 2), (turn_abs, 2), (turn_abs, 3), (turn_sign, 3), (turn_w, 0, 1), (turn_abs, 5), (turn_abs, 4), (turn_sign, 4), (turn_abs, 6), (turn_sign, 5), (first_matmul, 0, 0), (turn_abs, 7), (first_matmul, 0, 1), (column_sums, 1), (column_sums, 0), (turn_sign, 6), (turn_sign, 7), (turn_w, 0, 0), (first_matmul, 0, 3), (first_matmul, 0, 2), (turn_w, 0, 2), (first_matmul, 1, 0), (first_matmul, 1, 1), (first_matmul, 1, 2), (turn_w, 0, 3), (first_matmul, 1, 3), (turn_w, 1, 1), (turn_w, 1, 0), (second_matmul, 0, 0), (second_matmul, 1, 0), (second_matmul, 0, 1), (turn_w, 1, 3), (turn_w, 1, 2), (second_matmul, 1, 1), (second_matmul, 2, 1), (second_matmul, 2, 0), (turn_back, 0, 0), (turn_back, 0, 1), (second_matmul, 3, 0), (turn_back, 1, 1), (turn_back, 2, 1), (turn_back, 1, 0), (turn_back, 2, 0), (second_matmul, 3, 1), (second_matmul, 4, 0), (second_matmul, 4, 1), (second_matmul, 5, 0), (second_matmul, 5, 1), (turn_back, 3, 1), (turn_back, 3, 0), (turn_back, 4, 1), (turn_back, 4, 0), (turn_back, 5, 1), (turn_back, 5, 0), (second_matmul, 7, 0), (second_matmul, 6, 0), (second_matmul, 6, 1), (second_matmul, 7, 1), (turn_back, 6, 0), (turn_back, 6, 1), (turn_back, 7, 0), (turn_back, 7, 1)]

        counts = {}

        def real(step):
            return all(0 <= k < counts.get(step[0], STRIPS) for k in step[1:])

        queues = [[step for step in queue if real(step)] for queue in (vector, scalar, tensor)]
        done = set()
        while any(queues):
            moved = False
            for queue in queues:
                while queue and all(n in done or not real(n) for n in needs(queue[0])):
                    step = queue.pop(0)
                    step[0](*step[1:])
                    done.add(step)
                    moved = True
            assert moved
